import numpy as np
import ml_dtypes


def mxq(x, axis, fmt="e4m3"):
    dtype, down = {"e4m3": (ml_dtypes.float8_e4m3fn, 7), "e5m2": (ml_dtypes.float8_e5m2, 14)}[fmt]
    v = np.moveaxis(np.asarray(x, np.float32).astype(ml_dtypes.bfloat16).astype(np.float64), axis, -1)
    blocks = v.reshape(v.shape[:-1] + (-1, 32))
    amax = np.abs(blocks).max(-1, keepdims=True)
    byte = np.maximum(np.where(amax > 0, np.frexp(amax)[1] - 1 + 127, 0) - down, 1)
    scale = np.exp2(byte - 127.0)
    codes = (blocks / scale).astype(np.float32).astype(dtype).astype(np.float64)
    return np.moveaxis((codes * scale).reshape(v.shape), -1, axis)


WIDE = False


def mx_kscale(k):
    if not WIDE:
        return np.ones(k)
    levels = np.array([10, -10, 5, -5, 0])
    if k % 512:
        return np.exp2(np.random.permutation(np.resize(levels, k // 32))).repeat(32)
    a = np.empty((k // 512, 16))
    for p in range(k // 512):
        a[p, :8] = np.random.permutation(np.resize(levels, 8))
        for g in range(8):
            far = levels[np.abs(levels - a[p, g]) >= 10]
            a[p, g + 8] = far[np.random.randint(len(far))]
    return np.exp2(a.ravel()).repeat(32)


def f64(x):
    return np.asarray(x).astype(np.float64)


def striped(idx):
    return np.tile(idx.reshape(-1, 16).T, (8, 1)).astype(np.uint16)


def unstriped(offs):
    return offs[:16].T.reshape(-1).astype(np.int64)


E2M1 = np.array([0.0, 0.5, 1.0, 1.5, 2.0, 3.0, 4.0, 6.0, -0.0, -0.5, -1.0, -1.5, -2.0, -3.0, -4.0, -6.0])


def pack_weight(w, fmt):
    k, n = w.shape
    w = f64(np.asarray(w, np.float32).astype(ml_dtypes.bfloat16)).reshape(k // 32, 32, n)
    amax = np.abs(w).max(1)
    if fmt == "e4m3":
        byte = np.frexp(amax)[1] - 1 + 127 - 7
    else:
        mant, ex = np.frexp(amax / 6.0)
        byte = np.where(mant > 0.5, ex, ex - 1) + 127
    byte = np.clip(np.where(amax > 0, byte, 1), 1, 254)
    scaled = (w * np.exp2(127.0 - byte)[:, None, :]).reshape(k, n).astype(np.float32)
    by_word = np.ascontiguousarray(scaled.reshape(k // 512, 128, 4, n).transpose(0, 1, 3, 2))
    if fmt == "e4m3":
        words = by_word.astype(ml_dtypes.float8_e4m3fn).view(np.uint8)
    else:
        c = by_word.astype(ml_dtypes.float4_e2m1fn).view(np.uint8) & 0xF
        words = (c[..., 0::2] | (c[..., 1::2] << 4)).reshape(k // 512, 128, 2 * n)
    return np.ascontiguousarray(words), np.ascontiguousarray(byte.astype(np.uint8).reshape(k // 512, 16, n))


def unpack_weight(words, scales, fmt):
    g, _, n = scales.shape
    words = np.ascontiguousarray(words).reshape(g, 128, n, -1)
    if fmt == "e4m3":
        vals = words.view(ml_dtypes.float8_e4m3fn).astype(np.float64)
    else:
        nib = np.empty((g, 128, n, 4), np.uint8)
        nib[..., 0::2] = words & 0xF
        nib[..., 1::2] = words >> 4
        vals = E2M1[nib]
    vals = vals * np.repeat(np.exp2(scales.astype(np.float64) - 127.0), 8, axis=1)[..., None]
    return vals.transpose(0, 1, 3, 2).reshape(g * 512, n)


def relu(v):
    return np.maximum(v, 0.0)


K, T, E, C, H, N = 1536, 1536, 6, 256, 512, 512
R = 4


def by_expert(wq, xq):
    return np.concatenate([wq[e].T @ xq[:, e * C:(e + 1) * C] for e in range(E)], axis=1)


def setup_inputs():
    n = np.random.standard_normal
    s = mx_kscale(K)[:, None]
    u = mx_kscale(H)
    slot_token = np.concatenate([r * (T // R) + np.random.permutation(T // R)[:C // R] for e in range(E) for r in range(R)])
    x = pack_weight(n((K, T)) * s, "e4m3")
    return {
        "x_words": x[0],
        "x_scales": x[1],
        "w1": (n((E, K, H)) / np.sqrt(K) / s[None] * u[None, None, :]).astype(np.float32),
        "w2": (n((E, H, N)) / np.sqrt(H) / u[None, :, None]).astype(np.float32),
        "offs": striped(slot_token),
    }


def reference(x_words, x_scales, w1, w2, offs):
    idx = unstriped(offs)
    xq = unpack_weight(x_words, x_scales, "e4m3")[:, idx]
    h = relu(by_expert(mxq(f64(w1), 1, "e4m3"), xq))
    y = by_expert(mxq(f64(w2), 1, "e4m3"), mxq(h, 0, "e4m3"))
    return y.reshape(N, E, R, C // R).transpose(0, 2, 1, 3).reshape(N, E * C)

@@ -1,0 +1,163 @@
+from contextlib import ExitStack
+
+import concourse.mybir as mybir
+
+K, T, E, C, H, N = 1536, 1536, 6, 256, 512, 512
+R = 4
+FLOPS = 2 * E * C * (K * H + H * N)
+
+F32 = mybir.dt.float32
+BF16 = mybir.dt.bfloat16
+I32 = mybir.dt.int32
+U32 = mybir.dt.uint32
+U16 = mybir.dt.uint16
+U8 = mybir.dt.uint8
+FP8X4 = mybir.dt.float8_e4m3fn_x4
+RELU = mybir.ActivationFunctionType.Relu
+
+P = 128
+PACK = 4
+K_PASS = P * PACK
+PASSES = K // K_PASS
+U = C // R
+HALF = 128
+GROUPS = 128
+SCALAR_GROUPS = 72
+EARLY = 4
+
+
+def tile_moe_pke_mlp_relu_kernel(tc, x_words, x_scales, w1, w2, offs, out):
+    nc = tc.nc
+    with ExitStack() as ctx:
+        keep = ctx.enter_context(tc.tile_pool(name="keep", bufs=1))
+        raw_pool = ctx.enter_context(tc.tile_pool(name="raw", bufs=12))
+        bf_pool = ctx.enter_context(tc.tile_pool(name="bf", bufs=4))
+        code_pool = ctx.enter_context(tc.tile_pool(name="codes", bufs=8))
+        h_pool = ctx.enter_context(tc.tile_pool(name="h", bufs=2))
+        psum = ctx.enter_context(tc.psum_pool(name="psum", bufs=4))
+
+        offsets = keep.tile([P, E * C // 16], U16, name="offsets")
+        nc.sync.dma_start(offsets[:], offs)
+
+        token_scales = keep.tile([P, T // 4], I32, name="token_scales", align_bytes=64)
+        nc.vector.memset(token_scales[:], 0)
+        for q in range(4):
+            nc.gpsimd.dma_start(
+                out=token_scales[32 * q : 32 * q + 4 * PASSES, :],
+                in_=x_scales[:, 4 * q : 4 * q + 4, :].bitcast(I32),
+            )
+
+        token_words = [keep.tile([P, T], I32, name="token_words%d" % o, align_bytes=64) for o in range(PASSES)]
+        staged = [
+            keep.tile([P, 4, R, EARLY * U], F32, name="staged_early"),
+            keep.tile([P, 4, R, (E - EARLY) * U], F32, name="staged_late"),
+        ]
+
+        def load_tokens(o):
+            nc.sync.dma_start(
+                out=token_words[o][:], in_=x_words[o].rearrange("p t r -> p (t r)").bitcast(I32)
+            )
+
+        def load_rows(rows):
+            raw = raw_pool.tile([P, PACK, 512], F32, name="raw")
+            nc.sync.dma_start(out=raw[:], in_=rows.rearrange("(p j) w -> p j w", j=PACK))
+            return raw
+
+        def quantise_weights(raw, permute):
+            grouped = bf_pool.tile([P, 512 * PACK], BF16, name="grouped", align_bytes=64)
+            src = raw[:].rearrange("p j (g i) -> p g j i", i=4)
+            if permute:
+                dst = grouped[:].rearrange("p (i g j) -> p g j i", i=4, j=PACK)
+            else:
+                dst = grouped[:].rearrange("p (g i j) -> p g j i", i=4, j=PACK)
+            nc.scalar.copy(out=dst[:, :SCALAR_GROUPS], in_=src[:, :SCALAR_GROUPS])
+            nc.vector.tensor_copy(out=dst[:, SCALAR_GROUPS:], in_=src[:, SCALAR_GROUPS:])
+            codes = code_pool.tile([P, 512], U32, name="w_codes", align_bytes=64)
+            scales = code_pool.tile([P, 512], U8, name="w_scales", align_bytes=64)
+            nc.vector.quantize_mx(out=codes[:].bitcast(FP8X4), scales=scales[:], in_=grouped[:])
+            return codes, scales
+
+        def gather_words(e, o):
+            words = keep.tile([P, C], U32, name="slot_words%d_%d" % (e, o), align_bytes=64)
+            nc.vector.tensor_copy(
+                words[:], token_words[o][:].bitcast(U32).indirect(offsets[:, e * C // 16 : (e + 1) * C // 16])
+            )
+            return words
+
+        def gather_scales(e):
+            scales = keep.tile([P, C], U8, name="slot_scales%d" % e, align_bytes=64)
+            nc.vector.tensor_copy(
+                scales[:], token_scales[:].bitcast(U8).indirect(offsets[:, e * C // 16 : (e + 1) * C // 16])
+            )
+            return scales
+
+        def first_layer(e):
+            weights = []
+            words = []
+            for o in range(PASSES):
+                raw = load_rows(w1[e, o * K_PASS : (o + 1) * K_PASS, :])
+                if e == 0:
+                    load_tokens(o)
+                weights.append(quantise_weights(raw, True))
+                words.append(gather_words(e, o))
+            scales = gather_scales(e)
+            h = h_pool.tile([P, C, PACK], BF16, name="h", align_bytes=64)
+            for s0 in range(0, C, HALF):
+                acc = psum.tile([P, PACK, HALF], F32, name="acc_a")
+                for t in range(PACK):
+                    for o in range(PASSES):
+                        w_codes, w_scales = weights[o]
+                        nc.tensor.matmul_mx(
+                            out=acc[:, t, :],
+                            lhsT=w_codes[:, t * P : (t + 1) * P].bitcast(FP8X4),
+                            lhsT_scale=w_scales[:, t * P : (t + 1) * P],
+                            rhs=words[o][:, s0 : s0 + HALF].bitcast(FP8X4),
+                            rhs_scale=scales[4 * o :, s0 : s0 + HALF],
+                            start=(o == 0),
+                            stop=(o == PASSES - 1),
+                        )
+                nc.scalar.activation(out=h[:, s0 : s0 + HALF, :], in_=acc[:].rearrange("p t s -> p s t"), func=RELU)
+            h_codes = h_pool.tile([P, C], U32, name="h_codes", align_bytes=64)
+            h_scales = h_pool.tile([P, C], U8, name="h_scales", align_bytes=64)
+            nc.vector.quantize_mx(
+                out=h_codes[:].bitcast(FP8X4), scales=h_scales[:], in_=h[:].rearrange("p s t -> p (s t)")
+            )
+            return h_codes, h_scales
+
+        def second_layer(e, h_codes, h_scales):
+            w_codes, w_scales = quantise_weights(load_rows(w2[e]), False)
+            late = e >= EARLY
+            dest = staged[1] if late else staged[0]
+            u0 = (e - EARLY if late else e) * U
+            for b0 in range(0, 4, 2):
+                acc = psum.tile([P, 2, C], F32, name="acc_y")
+                for b in range(b0, b0 + 2):
+                    nc.tensor.matmul_mx(
+                        out=acc[:, b - b0, :],
+                        lhsT=w_codes[:, b * P : (b + 1) * P].bitcast(FP8X4),
+                        lhsT_scale=w_scales[:, b * P : (b + 1) * P],
+                        rhs=h_codes[:].bitcast(FP8X4),
+                        rhs_scale=h_scales[:],
+                        start=True,
+                        stop=True,
+                    )
+                y_out = dest[:, b0 : b0 + 2, :, u0 : u0 + U]
+                y_in = acc[:].rearrange("p b (m u) -> p b m u", m=R)
+                if e == E - 1 and b0 == 2:
+                    nc.vector.tensor_copy(out=y_out, in_=y_in)
+                else:
+                    nc.scalar.copy(out=y_out, in_=y_in)
+
+        hidden = {}
+        for e in range(E):
+            hidden[e] = first_layer(e)
+            if e < EARLY:
+                second_layer(e, *hidden[e])
+        for e in range(EARLY, E):
+            second_layer(e, *hidden[e])
+
+        by_rank = out.rearrange("(b p) (m c) -> b p m c", p=P, m=R)
+        for b in range(4):
+            nc.sync.dma_start(out=by_rank[b][:, :, : EARLY * U], in_=staged[0][:, b])
+        for b in range(4):
+            nc.sync.dma_start(out=by_rank[b][:, :, EARLY * U :], in_=staged[1][:, b])

@@ -22,15 +22,17 @@ PASSES = K // K_PASS
 U = C // R
 HALF = 128
 GROUPS = 128
-SCALAR_GROUPS = 72
+SCALAR_GROUPS = 80
+SCALAR_GROUPS_LATE = 44
 EARLY = 4
+RING = 13
 
 
 def tile_moe_pke_mlp_relu_kernel(tc, x_words, x_scales, w1, w2, offs, out):
     nc = tc.nc
     with ExitStack() as ctx:
         keep = ctx.enter_context(tc.tile_pool(name="keep", bufs=1))
-        raw_pool = ctx.enter_context(tc.tile_pool(name="raw", bufs=12))
+        ring = ctx.enter_context(tc.tile_pool(name="ring", bufs=1))
         bf_pool = ctx.enter_context(tc.tile_pool(name="bf", bufs=4))
         code_pool = ctx.enter_context(tc.tile_pool(name="codes", bufs=8))
         h_pool = ctx.enter_context(tc.tile_pool(name="h", bufs=2))
@@ -40,121 +42,194 @@ def tile_moe_pke_mlp_relu_kernel(tc, x_words, x_scales, w1, w2, offs, out):
         nc.sync.dma_start(offsets[:], offs)
 
         token_scales = keep.tile([P, T // 4], I32, name="token_scales", align_bytes=64)
+        landed_scales = keep.tile([P, T // 4], I32, name="landed_scales", align_bytes=64)
         nc.vector.memset(token_scales[:], 0)
-        for q in range(4):
-            nc.gpsimd.dma_start(
-                out=token_scales[32 * q : 32 * q + 4 * PASSES, :],
-                in_=x_scales[:, 4 * q : 4 * q + 4, :].bitcast(I32),
-            )
-
         token_words = [keep.tile([P, T], I32, name="token_words%d" % o, align_bytes=64) for o in range(PASSES)]
         staged = [
             keep.tile([P, 4, R, EARLY * U], F32, name="staged_early"),
             keep.tile([P, 4, R, (E - EARLY) * U], F32, name="staged_late"),
         ]
+        weights = {}
+        slot_words = {}
+        slot_scales = {}
+        sums = {}
+        hidden = {}
+        hidden_mx = {}
+
+        def in_slot(step, shape, dtype, name):
+            if step is None:
+                return keep.tile(shape, dtype, name=name, align_bytes=64)
+            return ring.tile(shape, dtype, name=name, tag="ring%d" % (step % RING), align_bytes=64)
+
+        def load_scales():
+            for q in range(4):
+                live = slice(32 * q, 32 * q + 4 * PASSES)
+                nc.sync.dma_start(out=landed_scales[live, :], in_=x_scales[:, 4 * q : 4 * q + 4, :].bitcast(I32))
+                nc.vector.tensor_copy(out=token_scales[live, :], in_=landed_scales[live, :])
 
         def load_tokens(o):
             nc.sync.dma_start(
                 out=token_words[o][:], in_=x_words[o].rearrange("p t r -> p (t r)").bitcast(I32)
             )
 
-        def load_rows(rows):
-            raw = raw_pool.tile([P, PACK, 512], F32, name="raw")
+        def load_rows(step, e, o):
+            rows = w1[e, o * K_PASS : (o + 1) * K_PASS, :] if o < PASSES else w2[e]
+            raw = in_slot(step, [P, PACK, 512], F32, "raw%d" % step)
             nc.sync.dma_start(out=raw[:], in_=rows.rearrange("(p j) w -> p j w", j=PACK))
             return raw
 
-        def quantise_weights(raw, permute):
+        def interleave(raw, permute, scalar_groups):
             grouped = bf_pool.tile([P, 512 * PACK], BF16, name="grouped", align_bytes=64)
             src = raw[:].rearrange("p j (g i) -> p g j i", i=4)
             if permute:
                 dst = grouped[:].rearrange("p (i g j) -> p g j i", i=4, j=PACK)
             else:
                 dst = grouped[:].rearrange("p (g i j) -> p g j i", i=4, j=PACK)
-            nc.scalar.copy(out=dst[:, :SCALAR_GROUPS], in_=src[:, :SCALAR_GROUPS])
-            nc.vector.tensor_copy(out=dst[:, SCALAR_GROUPS:], in_=src[:, SCALAR_GROUPS:])
+            if scalar_groups > 0:
+                nc.scalar.copy(out=dst[:, :scalar_groups], in_=src[:, :scalar_groups])
+            nc.vector.tensor_copy(out=dst[:, scalar_groups:], in_=src[:, scalar_groups:])
+            return grouped
+
+        def quantise_weights(e, o, grouped):
             codes = code_pool.tile([P, 512], U32, name="w_codes", align_bytes=64)
             scales = code_pool.tile([P, 512], U8, name="w_scales", align_bytes=64)
             nc.vector.quantize_mx(out=codes[:].bitcast(FP8X4), scales=scales[:], in_=grouped[:])
-            return codes, scales
+            weights[e, o] = (codes, scales)
 
-        def gather_words(e, o):
-            words = keep.tile([P, C], U32, name="slot_words%d_%d" % (e, o), align_bytes=64)
-            nc.vector.tensor_copy(
-                words[:], token_words[o][:].bitcast(U32).indirect(offsets[:, e * C // 16 : (e + 1) * C // 16])
-            )
-            return words
+        def gather_words(e, step):
+            words = in_slot(step, [P, 2, C], U32, "slot_words%d" % e)
+            for o in range(2):
+                nc.vector.tensor_copy(
+                    words[:, o, :],
+                    token_words[o][:].bitcast(U32).indirect(offsets[:, e * C // 16 : (e + 1) * C // 16]),
+                )
+                slot_words[e, o] = words[:, o, :]
 
-        def gather_scales(e):
-            scales = keep.tile([P, C], U8, name="slot_scales%d" % e, align_bytes=64)
-            nc.vector.tensor_copy(
-                scales[:], token_scales[:].bitcast(U8).indirect(offsets[:, e * C // 16 : (e + 1) * C // 16])
-            )
-            return scales
+        def gather_all(window, dtype, name):
+            parts = []
+            for first in range(0, E, 3):
+                part = keep.tile([P, 3 * C], dtype, name="%s%d" % (name, first), align_bytes=64)
+                nc.vector.tensor_copy(
+                    part[:], window[:].bitcast(dtype).indirect(offsets[:, first * C // 16 : (first + 3) * C // 16])
+                )
+                parts += [part[:, i * C : (i + 1) * C] for i in range(3)]
+            return parts
 
-        def first_layer(e):
-            weights = []
-            words = []
-            for o in range(PASSES):
-                raw = load_rows(w1[e, o * K_PASS : (o + 1) * K_PASS, :])
-                if e == 0:
-                    load_tokens(o)
-                weights.append(quantise_weights(raw, True))
-                words.append(gather_words(e, o))
-            scales = gather_scales(e)
-            h = h_pool.tile([P, C, PACK], BF16, name="h", align_bytes=64)
-            for s0 in range(0, C, HALF):
+        def first_products(e):
+            for half in range(2):
+                cols = slice(half * HALF, (half + 1) * HALF)
                 acc = psum.tile([P, PACK, HALF], F32, name="acc_a")
                 for t in range(PACK):
                     for o in range(PASSES):
-                        w_codes, w_scales = weights[o]
+                        w_codes, w_scales = weights[e, o]
                         nc.tensor.matmul_mx(
                             out=acc[:, t, :],
                             lhsT=w_codes[:, t * P : (t + 1) * P].bitcast(FP8X4),
                             lhsT_scale=w_scales[:, t * P : (t + 1) * P],
-                            rhs=words[o][:, s0 : s0 + HALF].bitcast(FP8X4),
-                            rhs_scale=scales[4 * o :, s0 : s0 + HALF],
+                            rhs=slot_words[e, o][:, cols].bitcast(FP8X4),
+                            rhs_scale=slot_scales[e][4 * o :, cols],
                             start=(o == 0),
                             stop=(o == PASSES - 1),
                         )
-                nc.scalar.activation(out=h[:, s0 : s0 + HALF, :], in_=acc[:].rearrange("p t s -> p s t"), func=RELU)
-            h_codes = h_pool.tile([P, C], U32, name="h_codes", align_bytes=64)
-            h_scales = h_pool.tile([P, C], U8, name="h_scales", align_bytes=64)
-            nc.vector.quantize_mx(
-                out=h_codes[:].bitcast(FP8X4), scales=h_scales[:], in_=h[:].rearrange("p s t -> p (s t)")
-            )
-            return h_codes, h_scales
+                sums[e, half] = acc
 
-        def second_layer(e, h_codes, h_scales):
-            w_codes, w_scales = quantise_weights(load_rows(w2[e]), False)
-            late = e >= EARLY
-            dest = staged[1] if late else staged[0]
-            u0 = (e - EARLY if late else e) * U
-            for b0 in range(0, 4, 2):
+        def relu(e, half, step):
+            hidden[e, half] = in_slot(step, [P, HALF, PACK], BF16, "hidden%d_%d" % (e, half))
+            nc.scalar.activation(out=hidden[e, half][:], in_=sums[e, half][:].rearrange("p t s -> p s t"), func=RELU)
+
+        def quantise_hidden(e, half, step=None):
+            if half == 0:
+                if step is None:
+                    h_codes = h_pool.tile([P, C], U32, name="h_codes", align_bytes=64)
+                else:
+                    h_codes = in_slot(step, [P, C], U32, "h_codes_last")
+                h_scales = h_pool.tile([P, C], U8, name="h_scales", align_bytes=64)
+                hidden_mx[e] = (h_codes, h_scales)
+            h_codes, h_scales = hidden_mx[e]
+            cols = slice(half * HALF, (half + 1) * HALF)
+            nc.vector.quantize_mx(
+                out=h_codes[:, cols].bitcast(FP8X4),
+                scales=h_scales[:, cols],
+                in_=hidden[e, half][:].rearrange("p s t -> p (s t)"),
+            )
+
+        def second_products(e):
+            w_codes, w_scales = weights[e, PASSES]
+            h_codes, h_scales = hidden_mx[e]
+            for pair in range(2):
                 acc = psum.tile([P, 2, C], F32, name="acc_y")
-                for b in range(b0, b0 + 2):
+                for b in range(2):
+                    cols = slice((2 * pair + b) * P, (2 * pair + b + 1) * P)
                     nc.tensor.matmul_mx(
-                        out=acc[:, b - b0, :],
-                        lhsT=w_codes[:, b * P : (b + 1) * P].bitcast(FP8X4),
-                        lhsT_scale=w_scales[:, b * P : (b + 1) * P],
+                        out=acc[:, b, :],
+                        lhsT=w_codes[:, cols].bitcast(FP8X4),
+                        lhsT_scale=w_scales[:, cols],
                         rhs=h_codes[:].bitcast(FP8X4),
                         rhs_scale=h_scales[:],
                         start=True,
                         stop=True,
                     )
-                y_out = dest[:, b0 : b0 + 2, :, u0 : u0 + U]
-                y_in = acc[:].rearrange("p b (m u) -> p b m u", m=R)
-                if e == E - 1 and b0 == 2:
-                    nc.vector.tensor_copy(out=y_out, in_=y_in)
-                else:
-                    nc.scalar.copy(out=y_out, in_=y_in)
+                sums[e, 2 + pair] = acc
 
-        hidden = {}
-        for e in range(E):
-            hidden[e] = first_layer(e)
-            if e < EARLY:
-                second_layer(e, *hidden[e])
-        for e in range(EARLY, E):
-            second_layer(e, *hidden[e])
+        def stage(e, pair, on_vector):
+            late = e >= EARLY
+            dest = staged[1] if late else staged[0]
+            u0 = (e - EARLY if late else e) * U
+            y_out = dest[:, 2 * pair : 2 * pair + 2, :, u0 : u0 + U]
+            y_in = sums[e, 2 + pair][:].rearrange("p b (m u) -> p b m u", m=R)
+            if on_vector:
+                nc.vector.tensor_copy(out=y_out, in_=y_in)
+            else:
+                nc.scalar.copy(out=y_out, in_=y_in)
+
+        pieces = [(e, o) for e in range(EARLY) for o in range(PASSES + 1)]
+        pieces += [(e, o) for e in range(EARLY, E) for o in range(PASSES)]
+        pieces += [(e, PASSES) for e in range(EARLY, E)]
+        last = len(pieces) - 1
+        ready = {e: pieces.index((e, PASSES - 1)) for e in range(E)}
+
+        load_tokens(2)
+        for step, (e, o) in enumerate(pieces):
+            raw = load_rows(step, e, o)
+            if step == 0:
+                load_scales()
+            if step < 2:
+                load_tokens(step)
+            if step == 2:
+                gather_words(0, None)
+                for d, part in enumerate(gather_all(token_words[2], U32, "last_words")):
+                    slot_words[d, 2] = part
+                for d, part in enumerate(gather_all(token_scales, U8, "slot_scales")):
+                    slot_scales[d] = part
+            share = SCALAR_GROUPS if step < last - 1 else SCALAR_GROUPS_LATE if step < last else 0
+            quantise_weights(e, o, interleave(raw, o < PASSES, share))
+            if o == PASSES - 1:
+                first_products(e)
+            for d in range(E - 1):
+                if step == ready[d] and d == EARLY:
+                    gather_words(d + 1, step)
+                if step == ready[d] + 2:
+                    relu(d, 0, step)
+                    quantise_hidden(d, 0)
+                if step == ready[d] + 3:
+                    relu(d, 1, step)
+                    quantise_hidden(d, 1)
+                    if d < EARLY:
+                        second_products(d)
+                        stage(d, 0, True)
+                        stage(d, 1, True)
+                        gather_words(d + 1, step)
+            if step == last - 1:
+                relu(E - 1, 0, step)
+                relu(E - 1, 1, None)
+                second_products(EARLY)
+                stage(EARLY, 0, False)
+                stage(EARLY, 1, False)
+        quantise_hidden(E - 1, 0, last)
+        quantise_hidden(E - 1, 1)
+        second_products(E - 1)
+        stage(E - 1, 0, True)
+        stage(E - 1, 1, False)
 
         by_rank = out.rearrange("(b p) (m c) -> b p m c", p=P, m=R)
         for b in range(4):

@@ -3,7 +3,7 @@ from contextlib import ExitStack
 import concourse.mybir as mybir
 
 K, T, E, C, H, N = 1536, 1536, 6, 256, 512, 512
-R = 4
+RANKS = 4
 FLOPS = 2 * E * C * (K * H + H * N)
 
 F32 = mybir.dt.float32
@@ -19,13 +19,20 @@ P = 128
 PACK = 4
 K_PASS = P * PACK
 PASSES = K // K_PASS
-U = C // R
-HALF = 128
-GROUPS = 128
-SCALAR_GROUPS = 80
-SCALAR_GROUPS_LATE = 44
+PER_RANK = C // RANKS
+HALF = C // 2
+ROW_BLOCKS = N // P
+LIST_GROUP = 16
+QUADRANT = 32
+
+SCALAR_GROUPS = 72
 EARLY = 4
+RELU_LAG = 3
+GATHER_EXPERTS = 3
 RING = 13
+ROUNDED_BUFS = 4
+CODE_BUFS = 8
+PSUM_BUFS = 4
 
 
 def tile_moe_pke_mlp_relu_kernel(tc, x_words, x_scales, w1, w2, offs, out):
@@ -33,12 +40,12 @@ def tile_moe_pke_mlp_relu_kernel(tc, x_words, x_scales, w1, w2, offs, out):
     with ExitStack() as ctx:
         keep = ctx.enter_context(tc.tile_pool(name="keep", bufs=1))
         ring = ctx.enter_context(tc.tile_pool(name="ring", bufs=1))
-        bf_pool = ctx.enter_context(tc.tile_pool(name="bf", bufs=4))
-        code_pool = ctx.enter_context(tc.tile_pool(name="codes", bufs=8))
-        h_pool = ctx.enter_context(tc.tile_pool(name="h", bufs=2))
-        psum = ctx.enter_context(tc.psum_pool(name="psum", bufs=4))
+        rounded_pool = ctx.enter_context(tc.tile_pool(name="rounded", bufs=ROUNDED_BUFS))
+        code_pool = ctx.enter_context(tc.tile_pool(name="codes", bufs=CODE_BUFS))
+        hidden_pool = ctx.enter_context(tc.tile_pool(name="hidden", bufs=2))
+        psum = ctx.enter_context(tc.psum_pool(name="psum", bufs=PSUM_BUFS))
 
-        offsets = keep.tile([P, E * C // 16], U16, name="offsets")
+        offsets = keep.tile([P, E * C // LIST_GROUP], U16, name="offsets")
         nc.sync.dma_start(offsets[:], offs)
 
         token_scales = keep.tile([P, T // 4], I32, name="token_scales", align_bytes=64)
@@ -46,73 +53,65 @@ def tile_moe_pke_mlp_relu_kernel(tc, x_words, x_scales, w1, w2, offs, out):
         nc.vector.memset(token_scales[:], 0)
         token_words = [keep.tile([P, T], I32, name="token_words%d" % o, align_bytes=64) for o in range(PASSES)]
         staged = [
-            keep.tile([P, 4, R, EARLY * U], F32, name="staged_early"),
-            keep.tile([P, 4, R, (E - EARLY) * U], F32, name="staged_late"),
+            keep.tile([P, ROW_BLOCKS, RANKS, EARLY * PER_RANK], F32, name="staged_early"),
+            keep.tile([P, ROW_BLOCKS, RANKS, (E - EARLY) * PER_RANK], F32, name="staged_late"),
         ]
         weights = {}
         slot_words = {}
         slot_scales = {}
-        sums = {}
+        first_sums = {}
+        second_sums = {}
         hidden = {}
         hidden_mx = {}
 
-        def in_slot(step, shape, dtype, name):
-            if step is None:
-                return keep.tile(shape, dtype, name=name, align_bytes=64)
+        def ring_tile(step, shape, dtype, name):
             return ring.tile(shape, dtype, name=name, tag="ring%d" % (step % RING), align_bytes=64)
 
+        def slots_of(first, count):
+            return offsets[:, first * C // LIST_GROUP : (first + count) * C // LIST_GROUP]
+
         def load_scales():
-            for q in range(4):
-                live = slice(32 * q, 32 * q + 4 * PASSES)
+            for q in range(P // QUADRANT):
+                live = slice(QUADRANT * q, QUADRANT * q + 4 * PASSES)
                 nc.sync.dma_start(out=landed_scales[live, :], in_=x_scales[:, 4 * q : 4 * q + 4, :].bitcast(I32))
                 nc.vector.tensor_copy(out=token_scales[live, :], in_=landed_scales[live, :])
 
         def load_tokens(o):
-            nc.sync.dma_start(
-                out=token_words[o][:], in_=x_words[o].rearrange("p t r -> p (t r)").bitcast(I32)
-            )
+            nc.sync.dma_start(out=token_words[o][:], in_=x_words[o].rearrange("p t r -> p (t r)").bitcast(I32))
 
-        def load_rows(step, e, o):
+        def load_piece(step, e, o, first, width):
             rows = w1[e, o * K_PASS : (o + 1) * K_PASS, :] if o < PASSES else w2[e]
-            raw = in_slot(step, [P, PACK, 512], F32, "raw%d" % step)
-            nc.sync.dma_start(out=raw[:], in_=rows.rearrange("(p j) w -> p j w", j=PACK))
+            raw = ring_tile(step, [P, PACK, width], F32, "raw%d" % step)
+            nc.sync.dma_start(out=raw[:], in_=rows.rearrange("(p j) w -> p j w", j=PACK)[:, :, first : first + width])
             return raw
 
-        def interleave(raw, permute, scalar_groups):
-            grouped = bf_pool.tile([P, 512 * PACK], BF16, name="grouped", align_bytes=64)
+        def quantise_piece(raw, permute, scalar_groups, width):
+            rounded = rounded_pool.tile([P, width * PACK], BF16, name="rounded", align_bytes=64)
             src = raw[:].rearrange("p j (g i) -> p g j i", i=4)
-            if permute:
-                dst = grouped[:].rearrange("p (i g j) -> p g j i", i=4, j=PACK)
-            else:
-                dst = grouped[:].rearrange("p (g i j) -> p g j i", i=4, j=PACK)
+            order = "p (i g j) -> p g j i" if permute else "p (g i j) -> p g j i"
+            dst = rounded[:].rearrange(order, i=4, j=PACK)
             if scalar_groups > 0:
                 nc.scalar.copy(out=dst[:, :scalar_groups], in_=src[:, :scalar_groups])
             nc.vector.tensor_copy(out=dst[:, scalar_groups:], in_=src[:, scalar_groups:])
-            return grouped
+            codes = code_pool.tile([P, width], U32, name="w_codes", align_bytes=64)
+            scales = code_pool.tile([P, width], U8, name="w_scales", align_bytes=64)
+            nc.vector.quantize_mx(out=codes[:].bitcast(FP8X4), scales=scales[:], in_=rounded[:])
+            return [(codes[:, c : c + P], scales[:, c : c + P]) for c in range(0, width, P)]
 
-        def quantise_weights(e, o, grouped):
-            codes = code_pool.tile([P, 512], U32, name="w_codes", align_bytes=64)
-            scales = code_pool.tile([P, 512], U8, name="w_scales", align_bytes=64)
-            nc.vector.quantize_mx(out=codes[:].bitcast(FP8X4), scales=scales[:], in_=grouped[:])
-            weights[e, o] = (codes, scales)
-
-        def gather_words(e, step):
-            words = in_slot(step, [P, 2, C], U32, "slot_words%d" % e)
-            for o in range(2):
-                nc.vector.tensor_copy(
-                    words[:, o, :],
-                    token_words[o][:].bitcast(U32).indirect(offsets[:, e * C // 16 : (e + 1) * C // 16]),
-                )
+        def gather_first_passes(e, words):
+            for o in range(PASSES - 1):
+                nc.vector.tensor_copy(words[:, o, :], token_words[o][:].bitcast(U32).indirect(slots_of(e, 1)))
                 slot_words[e, o] = words[:, o, :]
 
-        def gather_all(window, dtype, name):
+        def gather_first_passes_in_ring(e, step):
+            gather_first_passes(e, ring_tile(step, [P, PASSES - 1, C], U32, "slot_words%d" % e))
+
+        def gather_all_experts(window, dtype, name):
             parts = []
-            for first in range(0, E, 3):
-                part = keep.tile([P, 3 * C], dtype, name="%s%d" % (name, first), align_bytes=64)
-                nc.vector.tensor_copy(
-                    part[:], window[:].bitcast(dtype).indirect(offsets[:, first * C // 16 : (first + 3) * C // 16])
-                )
-                parts += [part[:, i * C : (i + 1) * C] for i in range(3)]
+            for first in range(0, E, GATHER_EXPERTS):
+                part = keep.tile([P, GATHER_EXPERTS * C], dtype, name="%s%d" % (name, first), align_bytes=64)
+                nc.vector.tensor_copy(part[:], window[:].bitcast(dtype).indirect(slots_of(first, GATHER_EXPERTS)))
+                parts += [part[:, i * C : (i + 1) * C] for i in range(GATHER_EXPERTS)]
             return parts
 
         def first_products(e):
@@ -121,118 +120,103 @@ def tile_moe_pke_mlp_relu_kernel(tc, x_words, x_scales, w1, w2, offs, out):
                 acc = psum.tile([P, PACK, HALF], F32, name="acc_a")
                 for t in range(PACK):
                     for o in range(PASSES):
-                        w_codes, w_scales = weights[e, o]
+                        w_codes, w_scales = weights[e, o][t]
                         nc.tensor.matmul_mx(
                             out=acc[:, t, :],
-                            lhsT=w_codes[:, t * P : (t + 1) * P].bitcast(FP8X4),
-                            lhsT_scale=w_scales[:, t * P : (t + 1) * P],
+                            lhsT=w_codes.bitcast(FP8X4),
+                            lhsT_scale=w_scales,
                             rhs=slot_words[e, o][:, cols].bitcast(FP8X4),
                             rhs_scale=slot_scales[e][4 * o :, cols],
                             start=(o == 0),
                             stop=(o == PASSES - 1),
                         )
-                sums[e, half] = acc
+                first_sums[e, half] = acc
 
-        def relu(e, half, step):
-            hidden[e, half] = in_slot(step, [P, HALF, PACK], BF16, "hidden%d_%d" % (e, half))
-            nc.scalar.activation(out=hidden[e, half][:], in_=sums[e, half][:].rearrange("p t s -> p s t"), func=RELU)
+        def relu(e, step):
+            hidden[e] = ring_tile(step, [P, 2, HALF, PACK], BF16, "hidden%d" % e)
+            for half in range(2):
+                nc.scalar.activation(
+                    out=hidden[e][:, half], in_=first_sums[e, half][:].rearrange("p t s -> p s t"), func=RELU
+                )
 
-        def quantise_hidden(e, half, step=None):
-            if half == 0:
-                if step is None:
-                    h_codes = h_pool.tile([P, C], U32, name="h_codes", align_bytes=64)
-                else:
-                    h_codes = in_slot(step, [P, C], U32, "h_codes_last")
-                h_scales = h_pool.tile([P, C], U8, name="h_scales", align_bytes=64)
-                hidden_mx[e] = (h_codes, h_scales)
-            h_codes, h_scales = hidden_mx[e]
-            cols = slice(half * HALF, (half + 1) * HALF)
-            nc.vector.quantize_mx(
-                out=h_codes[:, cols].bitcast(FP8X4),
-                scales=h_scales[:, cols],
-                in_=hidden[e, half][:].rearrange("p s t -> p (s t)"),
-            )
+        def quantise_hidden(e, h_codes):
+            h_scales = hidden_pool.tile([P, C], U8, name="h_scales", align_bytes=64)
+            for half in range(2):
+                cols = slice(half * HALF, (half + 1) * HALF)
+                nc.vector.quantize_mx(
+                    out=h_codes[:, cols].bitcast(FP8X4),
+                    scales=h_scales[:, cols],
+                    in_=hidden[e][:, half].rearrange("p s t -> p (s t)"),
+                )
+            hidden_mx[e] = (h_codes, h_scales)
 
         def second_products(e):
-            w_codes, w_scales = weights[e, PASSES]
             h_codes, h_scales = hidden_mx[e]
-            for pair in range(2):
+            for pair in range(ROW_BLOCKS // 2):
                 acc = psum.tile([P, 2, C], F32, name="acc_y")
                 for b in range(2):
-                    cols = slice((2 * pair + b) * P, (2 * pair + b + 1) * P)
+                    w_codes, w_scales = weights[e, PASSES][2 * pair + b]
                     nc.tensor.matmul_mx(
                         out=acc[:, b, :],
-                        lhsT=w_codes[:, cols].bitcast(FP8X4),
-                        lhsT_scale=w_scales[:, cols],
+                        lhsT=w_codes.bitcast(FP8X4),
+                        lhsT_scale=w_scales,
                         rhs=h_codes[:].bitcast(FP8X4),
                         rhs_scale=h_scales[:],
                         start=True,
                         stop=True,
                     )
-                sums[e, 2 + pair] = acc
+                second_sums[e, pair] = acc
 
-        def stage(e, pair, on_vector):
-            late = e >= EARLY
-            dest = staged[1] if late else staged[0]
-            u0 = (e - EARLY if late else e) * U
-            y_out = dest[:, 2 * pair : 2 * pair + 2, :, u0 : u0 + U]
-            y_in = sums[e, 2 + pair][:].rearrange("p b (m u) -> p b m u", m=R)
-            if on_vector:
-                nc.vector.tensor_copy(out=y_out, in_=y_in)
-            else:
-                nc.scalar.copy(out=y_out, in_=y_in)
+        def stage(e, copies):
+            group, place = (0, e) if e < EARLY else (1, e - EARLY)
+            for pair, copy in enumerate(copies):
+                copy(
+                    out=staged[group][:, 2 * pair : 2 * pair + 2, :, place * PER_RANK : (place + 1) * PER_RANK],
+                    in_=second_sums[e, pair][:].rearrange("p b (m u) -> p b m u", m=RANKS),
+                )
 
-        pieces = [(e, o) for e in range(EARLY) for o in range(PASSES + 1)]
-        pieces += [(e, o) for e in range(EARLY, E) for o in range(PASSES)]
-        pieces += [(e, PASSES) for e in range(EARLY, E)]
-        last = len(pieces) - 1
-        ready = {e: pieces.index((e, PASSES - 1)) for e in range(E)}
+        pieces = [(e, o, 0, H) for e in range(EARLY) for o in range(PASSES + 1)]
+        pieces += [(e, o, 0, H) for e in range(EARLY, E) for o in range(PASSES)]
+        pieces += [(E - 2, PASSES, 0, N), (E - 1, PASSES, 0, N // 2), (E - 1, PASSES, N // 2, N // 2)]
+        relu_step = {pieces.index((e, PASSES - 1, 0, H)) + RELU_LAG: e for e in range(E - 1)}
 
-        load_tokens(2)
-        for step, (e, o) in enumerate(pieces):
-            raw = load_rows(step, e, o)
+        load_tokens(PASSES - 1)
+        for step, (e, o, first, width) in enumerate(pieces):
+            raw = load_piece(step, e, o, first, width)
             if step == 0:
                 load_scales()
-            if step < 2:
+            if step < PASSES - 1:
                 load_tokens(step)
-            if step == 2:
-                gather_words(0, None)
-                for d, part in enumerate(gather_all(token_words[2], U32, "last_words")):
-                    slot_words[d, 2] = part
-                for d, part in enumerate(gather_all(token_scales, U8, "slot_scales")):
+            if step == PASSES - 1:
+                gather_first_passes(0, keep.tile([P, PASSES - 1, C], U32, name="slot_words0", align_bytes=64))
+                for d, part in enumerate(gather_all_experts(token_words[PASSES - 1], U32, "last_pass_words")):
+                    slot_words[d, PASSES - 1] = part
+                for d, part in enumerate(gather_all_experts(token_scales, U8, "slot_scales")):
                     slot_scales[d] = part
-            share = SCALAR_GROUPS if step < last - 1 else SCALAR_GROUPS_LATE if step < last else 0
-            quantise_weights(e, o, interleave(raw, o < PASSES, share))
+            scalar_groups = SCALAR_GROUPS if width == H else 0
+            weights.setdefault((e, o), []).extend(quantise_piece(raw, o < PASSES, scalar_groups, width))
             if o == PASSES - 1:
                 first_products(e)
-            for d in range(E - 1):
-                if step == ready[d] and d == EARLY:
-                    gather_words(d + 1, step)
-                if step == ready[d] + 2:
-                    relu(d, 0, step)
-                    quantise_hidden(d, 0)
-                if step == ready[d] + 3:
-                    relu(d, 1, step)
-                    quantise_hidden(d, 1)
-                    if d < EARLY:
-                        second_products(d)
-                        stage(d, 0, True)
-                        stage(d, 1, True)
-                        gather_words(d + 1, step)
-            if step == last - 1:
-                relu(E - 1, 0, step)
-                relu(E - 1, 1, None)
-                second_products(EARLY)
-                stage(EARLY, 0, False)
-                stage(EARLY, 1, False)
-        quantise_hidden(E - 1, 0, last)
-        quantise_hidden(E - 1, 1)
+            if (e, o) == (0, PASSES):
+                gather_first_passes_in_ring(1, step)
+            if step in relu_step:
+                d = relu_step[step]
+                relu(d, step)
+                quantise_hidden(d, hidden_pool.tile([P, C], U32, name="h_codes", align_bytes=64))
+                if d < EARLY:
+                    second_products(d)
+                    stage(d, [nc.scalar.copy, nc.vector.tensor_copy])
+                    gather_first_passes_in_ring(d + 2, step)
+            if (e, o) == (E - 2, PASSES):
+                relu(E - 1, step)
+                second_products(E - 2)
+                stage(E - 2, [nc.scalar.copy, nc.scalar.copy])
+        quantise_hidden(E - 1, ring_tile(len(pieces) - 1, [P, C], U32, "h_codes_last"))
         second_products(E - 1)
-        stage(E - 1, 0, True)
-        stage(E - 1, 1, False)
+        stage(E - 1, [nc.vector.tensor_copy, nc.scalar.copy])
 
-        by_rank = out.rearrange("(b p) (m c) -> b p m c", p=P, m=R)
-        for b in range(4):
-            nc.sync.dma_start(out=by_rank[b][:, :, : EARLY * U], in_=staged[0][:, b])
-        for b in range(4):
-            nc.sync.dma_start(out=by_rank[b][:, :, EARLY * U :], in_=staged[1][:, b])
+        by_rank = out.rearrange("(b p) (m c) -> b p m c", p=P, m=RANKS)
+        for b in range(ROW_BLOCKS):
+            nc.sync.dma_start(out=by_rank[b][:, :, : EARLY * PER_RANK], in_=staged[0][:, b])
+        for b in range(ROW_BLOCKS):
+            nc.sync.dma_start(out=by_rank[b][:, :, EARLY * PER_RANK :], in_=staged[1][:, b])

@@ -25,11 +25,11 @@ ROW_BLOCKS = N // P
 LIST_GROUP = 16
 QUADRANT = 32
 
-SCALAR_GROUPS = 72
+SCALAR_GROUPS = 76
 EARLY = 4
 RELU_LAG = 3
 GATHER_EXPERTS = 3
-RING = 13
+RING = 12
 ROUNDED_BUFS = 4
 CODE_BUFS = 8
 PSUM_BUFS = 4
@@ -42,7 +42,6 @@ def tile_moe_pke_mlp_relu_kernel(tc, x_words, x_scales, w1, w2, offs, out):
         ring = ctx.enter_context(tc.tile_pool(name="ring", bufs=1))
         rounded_pool = ctx.enter_context(tc.tile_pool(name="rounded", bufs=ROUNDED_BUFS))
         code_pool = ctx.enter_context(tc.tile_pool(name="codes", bufs=CODE_BUFS))
-        hidden_pool = ctx.enter_context(tc.tile_pool(name="hidden", bufs=2))
         psum = ctx.enter_context(tc.psum_pool(name="psum", bufs=PSUM_BUFS))
 
         offsets = keep.tile([P, E * C // LIST_GROUP], U16, name="offsets")
@@ -52,15 +51,13 @@ def tile_moe_pke_mlp_relu_kernel(tc, x_words, x_scales, w1, w2, offs, out):
         landed_scales = keep.tile([P, T // 4], I32, name="landed_scales", align_bytes=64)
         nc.vector.memset(token_scales[:], 0)
         token_words = [keep.tile([P, T], I32, name="token_words%d" % o, align_bytes=64) for o in range(PASSES)]
-        staged = [
-            keep.tile([P, ROW_BLOCKS, RANKS, EARLY * PER_RANK], F32, name="staged_early"),
-            keep.tile([P, ROW_BLOCKS, RANKS, (E - EARLY) * PER_RANK], F32, name="staged_late"),
-        ]
+        whole_rows = keep.tile([P, 2, RANKS, E * PER_RANK], F32, name="whole_rows")
+        early_rows = keep.tile([P, 2, RANKS, EARLY * PER_RANK], F32, name="early_rows")
+        late_rows = keep.tile([P, 2, RANKS, (E - EARLY) * PER_RANK], F32, name="late_rows")
         weights = {}
         slot_words = {}
         slot_scales = {}
         first_sums = {}
-        second_sums = {}
         hidden = {}
         hidden_mx = {}
 
@@ -79,20 +76,23 @@ def tile_moe_pke_mlp_relu_kernel(tc, x_words, x_scales, w1, w2, offs, out):
         def load_tokens(o):
             nc.sync.dma_start(out=token_words[o][:], in_=x_words[o].rearrange("p t r -> p (t r)").bitcast(I32))
 
-        def load_piece(step, e, o, first, width):
+        def load_piece(step, e, o):
             rows = w1[e, o * K_PASS : (o + 1) * K_PASS, :] if o < PASSES else w2[e]
-            raw = ring_tile(step, [P, PACK, width], F32, "raw%d" % step)
-            nc.sync.dma_start(out=raw[:], in_=rows.rearrange("(p j) w -> p j w", j=PACK)[:, :, first : first + width])
+            raw = ring_tile(step, [P, PACK, H], F32, "raw%d" % step)
+            nc.sync.dma_start(out=raw[:], in_=rows.rearrange("(p j) w -> p j w", j=PACK))
             return raw
 
-        def quantise_piece(raw, permute, scalar_groups, width):
+        def round_columns(raw, first, width, permute, scalar_groups):
             rounded = rounded_pool.tile([P, width * PACK], BF16, name="rounded", align_bytes=64)
-            src = raw[:].rearrange("p j (g i) -> p g j i", i=4)
+            src = raw[:, :, first : first + width].rearrange("p j (g i) -> p g j i", i=4)
             order = "p (i g j) -> p g j i" if permute else "p (g i j) -> p g j i"
             dst = rounded[:].rearrange(order, i=4, j=PACK)
             if scalar_groups > 0:
                 nc.scalar.copy(out=dst[:, :scalar_groups], in_=src[:, :scalar_groups])
             nc.vector.tensor_copy(out=dst[:, scalar_groups:], in_=src[:, scalar_groups:])
+            return rounded
+
+        def quantise(rounded, width):
             codes = code_pool.tile([P, width], U32, name="w_codes", align_bytes=64)
             scales = code_pool.tile([P, width], U8, name="w_scales", align_bytes=64)
             nc.vector.quantize_mx(out=codes[:].bitcast(FP8X4), scales=scales[:], in_=rounded[:])
@@ -140,49 +140,48 @@ def tile_moe_pke_mlp_relu_kernel(tc, x_words, x_scales, w1, w2, offs, out):
                 )
 
         def quantise_hidden(e, h_codes):
-            h_scales = hidden_pool.tile([P, C], U8, name="h_scales", align_bytes=64)
-            for half in range(2):
-                cols = slice(half * HALF, (half + 1) * HALF)
-                nc.vector.quantize_mx(
-                    out=h_codes[:, cols].bitcast(FP8X4),
-                    scales=h_scales[:, cols],
-                    in_=hidden[e][:, half].rearrange("p s t -> p (s t)"),
-                )
+            h_scales = keep.tile([P, C], U8, name="h_scales%d" % e, align_bytes=64)
+            nc.vector.quantize_mx(
+                out=h_codes[:].bitcast(FP8X4),
+                scales=h_scales[:],
+                in_=hidden[e][:].rearrange("p h s t -> p (h s t)"),
+            )
             hidden_mx[e] = (h_codes, h_scales)
 
-        def second_products(e):
+        def second_layer(e, blocks, w_tiles):
             h_codes, h_scales = hidden_mx[e]
-            for pair in range(ROW_BLOCKS // 2):
-                acc = psum.tile([P, 2, C], F32, name="acc_y")
-                for b in range(2):
-                    w_codes, w_scales = weights[e, PASSES][2 * pair + b]
-                    nc.tensor.matmul_mx(
-                        out=acc[:, b, :],
-                        lhsT=w_codes.bitcast(FP8X4),
-                        lhsT_scale=w_scales,
-                        rhs=h_codes[:].bitcast(FP8X4),
-                        rhs_scale=h_scales[:],
-                        start=True,
-                        stop=True,
-                    )
-                second_sums[e, pair] = acc
-
-        def stage(e, copies):
-            group, place = (0, e) if e < EARLY else (1, e - EARLY)
-            for pair, copy in enumerate(copies):
-                copy(
-                    out=staged[group][:, 2 * pair : 2 * pair + 2, :, place * PER_RANK : (place + 1) * PER_RANK],
-                    in_=second_sums[e, pair][:].rearrange("p b (m u) -> p b m u", m=RANKS),
+            acc = psum.tile([P, len(blocks), C], F32, name="acc_y")
+            for i, (w_codes, w_scales) in enumerate(w_tiles):
+                nc.tensor.matmul_mx(
+                    out=acc[:, i, :],
+                    lhsT=w_codes.bitcast(FP8X4),
+                    lhsT_scale=w_scales,
+                    rhs=h_codes[:].bitcast(FP8X4),
+                    rhs_scale=h_scales[:],
+                    start=True,
+                    stop=True,
                 )
+            if blocks[0] < 2:
+                staged, place = whole_rows, e
+            else:
+                staged, place = (early_rows, e) if e < EARLY else (late_rows, e - EARLY)
+            b = blocks[0] % 2
+            nc.scalar.copy(
+                out=staged[:, b : b + len(blocks), :, place * PER_RANK : (place + 1) * PER_RANK],
+                in_=acc[:].rearrange("p b (m u) -> p b m u", m=RANKS),
+            )
 
-        pieces = [(e, o, 0, H) for e in range(EARLY) for o in range(PASSES + 1)]
-        pieces += [(e, o, 0, H) for e in range(EARLY, E) for o in range(PASSES)]
-        pieces += [(E - 2, PASSES, 0, N), (E - 1, PASSES, 0, N // 2), (E - 1, PASSES, N // 2, N // 2)]
-        relu_step = {pieces.index((e, PASSES - 1, 0, H)) + RELU_LAG: e for e in range(E - 1)}
+        def second_layer_parts(e, raw, parts):
+            rounded = [round_columns(raw, blocks[0] * P, len(blocks) * P, False, 0) for blocks in parts]
+            for blocks, part in zip(parts, rounded):
+                second_layer(e, blocks, quantise(part, len(blocks) * P))
+
+        pieces = [(e, o) for e in range(E) for o in range(PASSES)] + [(e, PASSES) for e in range(E)]
+        relu_step = {pieces.index((e, PASSES - 1)) + (RELU_LAG if e < E - 1 else RELU_LAG - 1): e for e in range(E)}
 
         load_tokens(PASSES - 1)
-        for step, (e, o, first, width) in enumerate(pieces):
-            raw = load_piece(step, e, o, first, width)
+        for step, (e, o) in enumerate(pieces):
+            raw = load_piece(step, e, o)
             if step == 0:
                 load_scales()
             if step < PASSES - 1:
@@ -193,30 +192,33 @@ def tile_moe_pke_mlp_relu_kernel(tc, x_words, x_scales, w1, w2, offs, out):
                     slot_words[d, PASSES - 1] = part
                 for d, part in enumerate(gather_all_experts(token_scales, U8, "slot_scales")):
                     slot_scales[d] = part
-            scalar_groups = SCALAR_GROUPS if width == H else 0
-            weights.setdefault((e, o), []).extend(quantise_piece(raw, o < PASSES, scalar_groups, width))
+            if o < PASSES:
+                weights[e, o] = quantise(round_columns(raw, 0, H, True, SCALAR_GROUPS), H)
+            elif e < EARLY:
+                second_layer_parts(e, raw, [[2, 3], [0, 1]])
+            elif e < E - 1:
+                second_layer_parts(e, raw, [[0, 1], [2, 3]])
+            else:
+                second_layer_parts(e, raw, [[0], [1]])
+                second_layer_parts(e, raw, [[2, 3]])
             if o == PASSES - 1:
                 first_products(e)
-            if (e, o) == (0, PASSES):
+            if step == PASSES - 1:
                 gather_first_passes_in_ring(1, step)
             if step in relu_step:
                 d = relu_step[step]
                 relu(d, step)
-                quantise_hidden(d, hidden_pool.tile([P, C], U32, name="h_codes", align_bytes=64))
                 if d < EARLY:
-                    second_products(d)
-                    stage(d, [nc.scalar.copy, nc.vector.tensor_copy])
+                    quantise_hidden(d, keep.tile([P, C], U32, name="h_codes%d" % d, align_bytes=64))
                     gather_first_passes_in_ring(d + 2, step)
-            if (e, o) == (E - 2, PASSES):
-                relu(E - 1, step)
-                second_products(E - 2)
-                stage(E - 2, [nc.scalar.copy, nc.scalar.copy])
-        quantise_hidden(E - 1, ring_tile(len(pieces) - 1, [P, C], U32, "h_codes_last"))
-        second_products(E - 1)
-        stage(E - 1, [nc.vector.tensor_copy, nc.scalar.copy])
+            if relu_step.get(step - 1, 0) == E - 2 or relu_step.get(step - 2, 0) == E - 1:
+                d = E - 2 if relu_step.get(step - 1, 0) == E - 2 else E - 1
+                quantise_hidden(d, ring_tile(step, [P, C], U32, "h_codes%d" % d))
 
         by_rank = out.rearrange("(b p) (m c) -> b p m c", p=P, m=RANKS)
-        for b in range(ROW_BLOCKS):
-            nc.sync.dma_start(out=by_rank[b][:, :, : EARLY * PER_RANK], in_=staged[0][:, b])
-        for b in range(ROW_BLOCKS):
-            nc.sync.dma_start(out=by_rank[b][:, :, EARLY * PER_RANK :], in_=staged[1][:, b])
+        for b in range(2):
+            nc.sync.dma_start(out=by_rank[2 + b][:, :, : EARLY * PER_RANK], in_=early_rows[:, b])
+        for b in range(2):
+            nc.sync.dma_start(out=by_rank[b], in_=whole_rows[:, b])
+        for b in range(2):
+            nc.sync.dma_start(out=by_rank[2 + b][:, :, EARLY * PER_RANK :], in_=late_rows[:, b])

@@ -25,13 +25,18 @@ ROW_BLOCKS = N // P
 LIST_GROUP = 16
 QUADRANT = 32
 
-SCALAR_GROUPS = 76
+SCALAR_GROUPS = 70
 EARLY = 4
+WHOLE_BLOCKS = [0]
+SPLIT_BLOCKS = [2, 3, 1]
+WHOLE_LOADS = 5
+LATE_SCALAR_GROUPS = 56
+SLOT_BYTES = PACK * H * 4
 RELU_LAG = 3
 GATHER_EXPERTS = 3
-RING = 12
-ROUNDED_BUFS = 4
-CODE_BUFS = 8
+RING = 15
+ROUNDED_BUFS = 5
+CODE_BUFS = 10
 PSUM_BUFS = 4
 
 
@@ -50,10 +55,11 @@ def tile_moe_pke_mlp_relu_kernel(tc, x_words, x_scales, w1, w2, offs, out):
         token_scales = keep.tile([P, T // 4], I32, name="token_scales", align_bytes=64)
         landed_scales = keep.tile([P, T // 4], I32, name="landed_scales", align_bytes=64)
         nc.vector.memset(token_scales[:], 0)
-        token_words = [keep.tile([P, T], I32, name="token_words%d" % o, align_bytes=64) for o in range(PASSES)]
-        whole_rows = keep.tile([P, 2, RANKS, E * PER_RANK], F32, name="whole_rows")
-        early_rows = keep.tile([P, 2, RANKS, EARLY * PER_RANK], F32, name="early_rows")
-        late_rows = keep.tile([P, 2, RANKS, (E - EARLY) * PER_RANK], F32, name="late_rows")
+        first_words = keep.tile([P, PASSES - 1, T], I32, name="first_words", align_bytes=64)
+        last_words = keep.tile([P, T], I32, name="last_words", align_bytes=64)
+        token_words = [first_words[:, o, :] for o in range(PASSES - 1)] + [last_words[:]]
+        staged = keep.tile([P, ROW_BLOCKS, RANKS, E * PER_RANK], F32, name="staged")
+        by_rank = out.rearrange("(b p) (m c) -> b p m c", p=P, m=RANKS)
         weights = {}
         slot_words = {}
         slot_scales = {}
@@ -62,7 +68,7 @@ def tile_moe_pke_mlp_relu_kernel(tc, x_words, x_scales, w1, w2, offs, out):
         hidden_mx = {}
 
         def ring_tile(step, shape, dtype, name):
-            return ring.tile(shape, dtype, name=name, tag="ring%d" % (step % RING), align_bytes=64)
+            return ring.tile(shape, dtype, name=name, offset=(step % RING) * SLOT_BYTES, align_bytes=64)
 
         def slots_of(first, count):
             return offsets[:, first * C // LIST_GROUP : (first + count) * C // LIST_GROUP]
@@ -73,14 +79,16 @@ def tile_moe_pke_mlp_relu_kernel(tc, x_words, x_scales, w1, w2, offs, out):
                 nc.sync.dma_start(out=landed_scales[live, :], in_=x_scales[:, 4 * q : 4 * q + 4, :].bitcast(I32))
                 nc.vector.tensor_copy(out=token_scales[live, :], in_=landed_scales[live, :])
 
-        def load_tokens(o):
-            nc.sync.dma_start(out=token_words[o][:], in_=x_words[o].rearrange("p t r -> p (t r)").bitcast(I32))
+        def load_expert(step, e):
+            raw = ring_tile(step, [P, PASSES, PACK, H], F32, "raw%d" % step)
+            nc.sync.dma_start(out=raw[:], in_=w1[e].rearrange("(o p j) w -> p o j w", p=P, j=PACK))
+            return [raw[:, o] for o in range(PASSES)]
 
         def load_piece(step, e, o):
             rows = w1[e, o * K_PASS : (o + 1) * K_PASS, :] if o < PASSES else w2[e]
             raw = ring_tile(step, [P, PACK, H], F32, "raw%d" % step)
             nc.sync.dma_start(out=raw[:], in_=rows.rearrange("(p j) w -> p j w", j=PACK))
-            return raw
+            return raw[:]
 
         def round_columns(raw, first, width, permute, scalar_groups):
             rounded = rounded_pool.tile([P, width * PACK], BF16, name="rounded", align_bytes=64)
@@ -100,7 +108,7 @@ def tile_moe_pke_mlp_relu_kernel(tc, x_words, x_scales, w1, w2, offs, out):
 
         def gather_first_passes(e, words):
             for o in range(PASSES - 1):
-                nc.vector.tensor_copy(words[:, o, :], token_words[o][:].bitcast(U32).indirect(slots_of(e, 1)))
+                nc.vector.tensor_copy(words[:, o, :], token_words[o].bitcast(U32).indirect(slots_of(e, 1)))
                 slot_words[e, o] = words[:, o, :]
 
         def gather_first_passes_in_ring(e, step):
@@ -110,7 +118,7 @@ def tile_moe_pke_mlp_relu_kernel(tc, x_words, x_scales, w1, w2, offs, out):
             parts = []
             for first in range(0, E, GATHER_EXPERTS):
                 part = keep.tile([P, GATHER_EXPERTS * C], dtype, name="%s%d" % (name, first), align_bytes=64)
-                nc.vector.tensor_copy(part[:], window[:].bitcast(dtype).indirect(slots_of(first, GATHER_EXPERTS)))
+                nc.vector.tensor_copy(part[:], window.bitcast(dtype).indirect(slots_of(first, GATHER_EXPERTS)))
                 parts += [part[:, i * C : (i + 1) * C] for i in range(GATHER_EXPERTS)]
             return parts
 
@@ -161,15 +169,15 @@ def tile_moe_pke_mlp_relu_kernel(tc, x_words, x_scales, w1, w2, offs, out):
                     start=True,
                     stop=True,
                 )
-            if blocks[0] < 2:
-                staged, place = whole_rows, e
-            else:
-                staged, place = (early_rows, e) if e < EARLY else (late_rows, e - EARLY)
-            b = blocks[0] % 2
             nc.scalar.copy(
-                out=staged[:, b : b + len(blocks), :, place * PER_RANK : (place + 1) * PER_RANK],
+                out=staged[:, blocks[0] : blocks[0] + len(blocks), :, e * PER_RANK : (e + 1) * PER_RANK],
                 in_=acc[:].rearrange("p b (m u) -> p b m u", m=RANKS),
             )
+
+        def store(blocks, first, last):
+            cols = slice(first * PER_RANK, last * PER_RANK)
+            for b in blocks:
+                nc.sync.dma_start(out=by_rank[b][:, :, cols], in_=staged[:, b, :, cols])
 
         def second_layer_parts(e, raw, parts):
             rounded = [round_columns(raw, blocks[0] * P, len(blocks) * P, False, 0) for blocks in parts]
@@ -179,23 +187,31 @@ def tile_moe_pke_mlp_relu_kernel(tc, x_words, x_scales, w1, w2, offs, out):
         pieces = [(e, o) for e in range(E) for o in range(PASSES)] + [(e, PASSES) for e in range(E)]
         relu_step = {pieces.index((e, PASSES - 1)) + (RELU_LAG if e < E - 1 else RELU_LAG - 1): e for e in range(E)}
 
-        load_tokens(PASSES - 1)
+        packed = x_words.rearrange("o p t r -> p o (t r)").bitcast(I32)
+        nc.sync.dma_start(out=last_words[:], in_=packed[:, PASSES - 1])
+        nc.sync.dma_start(out=first_words[:], in_=packed[:, : PASSES - 1])
+        load_scales()
         for step, (e, o) in enumerate(pieces):
-            raw = load_piece(step, e, o)
-            if step == 0:
-                load_scales()
-            if step < PASSES - 1:
-                load_tokens(step)
+            if step >= WHOLE_LOADS * PASSES:
+                raw = load_piece(step, e, o)
+            else:
+                if o == 0:
+                    raws = load_expert(step, e)
+                raw = raws[o]
             if step == PASSES - 1:
                 gather_first_passes(0, keep.tile([P, PASSES - 1, C], U32, name="slot_words0", align_bytes=64))
                 for d, part in enumerate(gather_all_experts(token_words[PASSES - 1], U32, "last_pass_words")):
                     slot_words[d, PASSES - 1] = part
-                for d, part in enumerate(gather_all_experts(token_scales, U8, "slot_scales")):
+                for d, part in enumerate(gather_all_experts(token_scales[:], U8, "slot_scales")):
                     slot_scales[d] = part
             if o < PASSES:
-                weights[e, o] = quantise(round_columns(raw, 0, H, True, SCALAR_GROUPS), H)
-            elif e < EARLY:
-                second_layer_parts(e, raw, [[2, 3], [0, 1]])
+                weights[e, o] = quantise(round_columns(raw, 0, H, True, SCALAR_GROUPS if e < EARLY else LATE_SCALAR_GROUPS), H)
+            elif e < EARLY - 1:
+                second_layer_parts(e, raw, [[0, 1], [2, 3]])
+            elif e == EARLY - 1:
+                second_layer_parts(e, raw, [[2], [3]])
+                second_layer_parts(e, raw, [[0, 1]])
+                store(SPLIT_BLOCKS, 0, EARLY)
             elif e < E - 1:
                 second_layer_parts(e, raw, [[0, 1], [2, 3]])
             else:
@@ -215,10 +231,5 @@ def tile_moe_pke_mlp_relu_kernel(tc, x_words, x_scales, w1, w2, offs, out):
                 d = E - 2 if relu_step.get(step - 1, 0) == E - 2 else E - 1
                 quantise_hidden(d, ring_tile(step, [P, C], U32, "h_codes%d" % d))
 
-        by_rank = out.rearrange("(b p) (m c) -> b p m c", p=P, m=RANKS)
-        for b in range(2):
-            nc.sync.dma_start(out=by_rank[2 + b][:, :, : EARLY * PER_RANK], in_=early_rows[:, b])
-        for b in range(2):
-            nc.sync.dma_start(out=by_rank[b], in_=whole_rows[:, b])
-        for b in range(2):
-            nc.sync.dma_start(out=by_rank[2 + b][:, :, EARLY * PER_RANK :], in_=late_rows[:, b])
+        store(WHOLE_BLOCKS, 0, E)
+        store(sorted(SPLIT_BLOCKS), EARLY, E)

@@ -25,18 +25,18 @@ ROW_BLOCKS = N // P
 LIST_GROUP = 16
 QUADRANT = 32
 
-SCALAR_GROUPS = 70
+SCALAR_GROUPS = 68
 EARLY = 4
 WHOLE_BLOCKS = [0]
 SPLIT_BLOCKS = [2, 3, 1]
-WHOLE_LOADS = 5
-LATE_SCALAR_GROUPS = 56
+WHOLE_LOADS = 4
+LATE_SCALAR_GROUPS = 64
 SLOT_BYTES = PACK * H * 4
 RELU_LAG = 3
 GATHER_EXPERTS = 3
 RING = 15
 ROUNDED_BUFS = 5
-CODE_BUFS = 10
+CODE_BUFS = 9
 PSUM_BUFS = 4
 
 
@@ -106,21 +106,10 @@ def tile_moe_pke_mlp_relu_kernel(tc, x_words, x_scales, w1, w2, offs, out):
             nc.vector.quantize_mx(out=codes[:].bitcast(FP8X4), scales=scales[:], in_=rounded[:])
             return [(codes[:, c : c + P], scales[:, c : c + P]) for c in range(0, width, P)]
 
-        def gather_first_passes(e, words):
-            for o in range(PASSES - 1):
-                nc.vector.tensor_copy(words[:, o, :], token_words[o].bitcast(U32).indirect(slots_of(e, 1)))
-                slot_words[e, o] = words[:, o, :]
-
-        def gather_first_passes_in_ring(e, step):
-            gather_first_passes(e, ring_tile(step, [P, PASSES - 1, C], U32, "slot_words%d" % e))
-
-        def gather_all_experts(window, dtype, name):
-            parts = []
-            for first in range(0, E, GATHER_EXPERTS):
-                part = keep.tile([P, GATHER_EXPERTS * C], dtype, name="%s%d" % (name, first), align_bytes=64)
-                nc.vector.tensor_copy(part[:], window.bitcast(dtype).indirect(slots_of(first, GATHER_EXPERTS)))
-                parts += [part[:, i * C : (i + 1) * C] for i in range(GATHER_EXPERTS)]
-            return parts
+        def gather(window, dtype, first, name):
+            part = keep.tile([P, GATHER_EXPERTS * C], dtype, name="%s_%d" % (name, first), align_bytes=64)
+            nc.vector.tensor_copy(part[:], window.bitcast(dtype).indirect(slots_of(first, GATHER_EXPERTS)))
+            return {first + i: part[:, i * C : (i + 1) * C] for i in range(GATHER_EXPERTS)}
 
         def first_products(e):
             for half in range(2):
@@ -191,6 +180,12 @@ def tile_moe_pke_mlp_relu_kernel(tc, x_words, x_scales, w1, w2, offs, out):
         nc.sync.dma_start(out=last_words[:], in_=packed[:, PASSES - 1])
         nc.sync.dma_start(out=first_words[:], in_=packed[:, : PASSES - 1])
         load_scales()
+        for first in range(0, E, GATHER_EXPERTS):
+            for o in range(PASSES):
+                for e, part in gather(token_words[o], U32, first, "slot_words%d" % o).items():
+                    slot_words[e, o] = part
+            for e, part in gather(token_scales[:], U8, first, "slot_scales").items():
+                slot_scales[e] = part
         for step, (e, o) in enumerate(pieces):
             if step >= WHOLE_LOADS * PASSES:
                 raw = load_piece(step, e, o)
@@ -198,14 +193,8 @@ def tile_moe_pke_mlp_relu_kernel(tc, x_words, x_scales, w1, w2, offs, out):
                 if o == 0:
                     raws = load_expert(step, e)
                 raw = raws[o]
-            if step == PASSES - 1:
-                gather_first_passes(0, keep.tile([P, PASSES - 1, C], U32, name="slot_words0", align_bytes=64))
-                for d, part in enumerate(gather_all_experts(token_words[PASSES - 1], U32, "last_pass_words")):
-                    slot_words[d, PASSES - 1] = part
-                for d, part in enumerate(gather_all_experts(token_scales[:], U8, "slot_scales")):
-                    slot_scales[d] = part
             if o < PASSES:
-                weights[e, o] = quantise(round_columns(raw, 0, H, True, SCALAR_GROUPS if e < EARLY else LATE_SCALAR_GROUPS), H)
+                weights[e, o] = quantise(round_columns(raw, 0, H, True, SCALAR_GROUPS if e < WHOLE_LOADS - 1 else LATE_SCALAR_GROUPS), H)
             elif e < EARLY - 1:
                 second_layer_parts(e, raw, [[0, 1], [2, 3]])
             elif e == EARLY - 1:
@@ -219,14 +208,11 @@ def tile_moe_pke_mlp_relu_kernel(tc, x_words, x_scales, w1, w2, offs, out):
                 second_layer_parts(e, raw, [[2, 3]])
             if o == PASSES - 1:
                 first_products(e)
-            if step == PASSES - 1:
-                gather_first_passes_in_ring(1, step)
             if step in relu_step:
                 d = relu_step[step]
                 relu(d, step)
                 if d < EARLY:
                     quantise_hidden(d, keep.tile([P, C], U32, name="h_codes%d" % d, align_bytes=64))
-                    gather_first_passes_in_ring(d + 2, step)
             if relu_step.get(step - 1, 0) == E - 2 or relu_step.get(step - 2, 0) == E - 1:
                 d = E - 2 if relu_step.get(step - 1, 0) == E - 2 else E - 1
                 quantise_hidden(d, ring_tile(step, [P, C], U32, "h_codes%d" % d))

@@ -25,14 +25,15 @@ ROW_BLOCKS = N // P
 LIST_GROUP = 16
 QUADRANT = 32
 
+GROUP = 4
+SLOT_BYTES = PACK * H * 4
+
 SCALAR_GROUPS = 68
 EARLY = 4
 WHOLE_BLOCKS = [0]
 SPLIT_BLOCKS = [2, 3, 1]
-WHOLE_LOADS = 4
-LATE_SCALAR_GROUPS = 64
-SLOT_BYTES = PACK * H * 4
-RELU_LAG = 3
+WHOLE_LOADS = 5
+PROMPT_RELUS = 3
 GATHER_EXPERTS = 3
 RING = 15
 ROUNDED_BUFS = 5
@@ -67,8 +68,8 @@ def tile_moe_pke_mlp_relu_kernel(tc, x_words, x_scales, w1, w2, offs, out):
         hidden = {}
         hidden_mx = {}
 
-        def ring_tile(step, shape, dtype, name):
-            return ring.tile(shape, dtype, name=name, offset=(step % RING) * SLOT_BYTES, align_bytes=64)
+        def ring_tile(step, shape, dtype, name, start=0):
+            return ring.tile(shape, dtype, name=name, offset=(step % RING) * SLOT_BYTES + start, align_bytes=64)
 
         def slots_of(first, count):
             return offsets[:, first * C // LIST_GROUP : (first + count) * C // LIST_GROUP]
@@ -92,9 +93,9 @@ def tile_moe_pke_mlp_relu_kernel(tc, x_words, x_scales, w1, w2, offs, out):
 
         def round_columns(raw, first, width, permute, scalar_groups):
             rounded = rounded_pool.tile([P, width * PACK], BF16, name="rounded", align_bytes=64)
-            src = raw[:, :, first : first + width].rearrange("p j (g i) -> p g j i", i=4)
+            src = raw[:, :, first : first + width].rearrange("p j (g i) -> p g j i", i=GROUP)
             order = "p (i g j) -> p g j i" if permute else "p (g i j) -> p g j i"
-            dst = rounded[:].rearrange(order, i=4, j=PACK)
+            dst = rounded[:].rearrange(order, i=GROUP, j=PACK)
             if scalar_groups > 0:
                 nc.scalar.copy(out=dst[:, :scalar_groups], in_=src[:, :scalar_groups])
             nc.vector.tensor_copy(out=dst[:, scalar_groups:], in_=src[:, scalar_groups:])
@@ -174,7 +175,11 @@ def tile_moe_pke_mlp_relu_kernel(tc, x_words, x_scales, w1, w2, offs, out):
                 second_layer(e, blocks, quantise(part, len(blocks) * P))
 
         pieces = [(e, o) for e in range(E) for o in range(PASSES)] + [(e, PASSES) for e in range(E)]
-        relu_step = {pieces.index((e, PASSES - 1)) + (RELU_LAG if e < E - 1 else RELU_LAG - 1): e for e in range(E)}
+        last_w1 = E * PASSES - 1
+        relu_step = {pieces.index((e + 1, PASSES - 1)): e for e in range(PROMPT_RELUS)}
+        for e in range(PROMPT_RELUS, E):
+            relu_step[last_w1 + e - PROMPT_RELUS] = e
+        late_hidden = {step + (1 if e < E - 1 else 2): e for step, e in relu_step.items() if e >= PROMPT_RELUS}
 
         packed = x_words.rearrange("o p t r -> p o (t r)").bitcast(I32)
         nc.sync.dma_start(out=last_words[:], in_=packed[:, PASSES - 1])
@@ -186,36 +191,35 @@ def tile_moe_pke_mlp_relu_kernel(tc, x_words, x_scales, w1, w2, offs, out):
                     slot_words[e, o] = part
             for e, part in gather(token_scales[:], U8, first, "slot_scales").items():
                 slot_scales[e] = part
+
         for step, (e, o) in enumerate(pieces):
-            if step >= WHOLE_LOADS * PASSES:
+            if e >= WHOLE_LOADS or o == PASSES:
                 raw = load_piece(step, e, o)
             else:
                 if o == 0:
-                    raws = load_expert(step, e)
-                raw = raws[o]
+                    expert_pieces = load_expert(step, e)
+                raw = expert_pieces[o]
             if o < PASSES:
-                weights[e, o] = quantise(round_columns(raw, 0, H, True, SCALAR_GROUPS if e < WHOLE_LOADS - 1 else LATE_SCALAR_GROUPS), H)
-            elif e < EARLY - 1:
-                second_layer_parts(e, raw, [[0, 1], [2, 3]])
+                weights[e, o] = quantise(round_columns(raw, 0, H, True, SCALAR_GROUPS), H)
             elif e == EARLY - 1:
                 second_layer_parts(e, raw, [[2], [3]])
                 second_layer_parts(e, raw, [[0, 1]])
                 store(SPLIT_BLOCKS, 0, EARLY)
-            elif e < E - 1:
-                second_layer_parts(e, raw, [[0, 1], [2, 3]])
-            else:
+            elif e == E - 1:
                 second_layer_parts(e, raw, [[0], [1]])
                 second_layer_parts(e, raw, [[2, 3]])
-            if o == PASSES - 1:
-                first_products(e)
+            else:
+                second_layer_parts(e, raw, [[0, 1], [2, 3]])
             if step in relu_step:
                 d = relu_step[step]
                 relu(d, step)
-                if d < EARLY:
+                if d < PROMPT_RELUS:
                     quantise_hidden(d, keep.tile([P, C], U32, name="h_codes%d" % d, align_bytes=64))
-            if relu_step.get(step - 1, 0) == E - 2 or relu_step.get(step - 2, 0) == E - 1:
-                d = E - 2 if relu_step.get(step - 1, 0) == E - 2 else E - 1
-                quantise_hidden(d, ring_tile(step, [P, C], U32, "h_codes%d" % d))
+            if o == PASSES - 1:
+                first_products(e)
+            if step in late_hidden:
+                d = late_hidden[step]
+                quantise_hidden(d, ring_tile(step, [P, C], U32, "h_codes%d" % d, SLOT_BYTES // 2))
 
         store(WHOLE_BLOCKS, 0, E)
         store(sorted(SPLIT_BLOCKS), EARLY, E)

@@ -78,6 +78,10 @@ def tile_moe_pke_mlp_relu_kernel(tc, x_words, x_scales, w1, w2, offs, out):
             for q in range(P // QUADRANT):
                 live = slice(QUADRANT * q, QUADRANT * q + 4 * PASSES)
                 nc.sync.dma_start(out=landed_scales[live, :], in_=x_scales[:, 4 * q : 4 * q + 4, :].bitcast(I32))
+
+        def move_scales():
+            for q in range(P // QUADRANT):
+                live = slice(QUADRANT * q, QUADRANT * q + 4 * PASSES)
                 nc.vector.tensor_copy(out=token_scales[live, :], in_=landed_scales[live, :])
 
         def load_expert(step, e):
@@ -185,10 +189,12 @@ def tile_moe_pke_mlp_relu_kernel(tc, x_words, x_scales, w1, w2, offs, out):
         nc.sync.dma_start(out=last_words[:], in_=packed[:, PASSES - 1])
         nc.sync.dma_start(out=first_words[:], in_=packed[:, : PASSES - 1])
         load_scales()
-        for first in range(0, E, GATHER_EXPERTS):
-            for o in range(PASSES):
+        for o in reversed(range(PASSES)):
+            for first in range(0, E, GATHER_EXPERTS):
                 for e, part in gather(token_words[o], U32, first, "slot_words%d" % o).items():
                     slot_words[e, o] = part
+        move_scales()
+        for first in range(0, E, GATHER_EXPERTS):
             for e, part in gather(token_scales[:], U8, first, "slot_scales").items():
                 slot_scales[e] = part
 

@@ -77,7 +77,7 @@ def tile_moe_pke_mlp_relu_kernel(tc, x_words, x_scales, w1, w2, offs, out):
         def load_scales():
             for q in range(P // QUADRANT):
                 live = slice(QUADRANT * q, QUADRANT * q + 4 * PASSES)
-                nc.sync.dma_start(out=landed_scales[live, :], in_=x_scales[:, 4 * q : 4 * q + 4, :].bitcast(I32))
+                nc.gpsimd.dma_start(out=landed_scales[live, :], in_=x_scales[:, 4 * q : 4 * q + 4, :].bitcast(I32))
 
         def move_scales():
             for q in range(P // QUADRANT):

@@ -27,6 +27,10 @@ QUADRANT = 32
 
 GROUP = 4
 SLOT_BYTES = PACK * H * 4
+WORD_BYTES = T * 4
+STAGED_BYTES = ROW_BLOCKS * E * C * 4
+ROW_ALIGN = 2048
+LIST_ALIGN = 256
 
 SCALAR_GROUPS = 68
 EARLY = 4
@@ -50,16 +54,19 @@ def tile_moe_pke_mlp_relu_kernel(tc, x_words, x_scales, w1, w2, offs, out):
         code_pool = ctx.enter_context(tc.tile_pool(name="codes", bufs=CODE_BUFS))
         psum = ctx.enter_context(tc.psum_pool(name="psum", bufs=PSUM_BUFS))
 
-        offsets = keep.tile([P, E * C // LIST_GROUP], U16, name="offsets")
+        def dma_tile(shape, dtype, name, start):
+            return ring.tile(shape, dtype, name=name, offset=RING * SLOT_BYTES + start, align_bytes=ROW_ALIGN)
+
+        offsets = keep.tile([P, E * C // LIST_GROUP], U16, name="offsets", align_bytes=LIST_ALIGN)
         nc.sync.dma_start(offsets[:], offs)
 
         token_scales = keep.tile([P, T // 4], I32, name="token_scales", align_bytes=64)
-        landed_scales = keep.tile([P, T // 4], I32, name="landed_scales", align_bytes=64)
+        landed_scales = dma_tile([P, T // 4], I32, "landed_scales", STAGED_BYTES + PASSES * WORD_BYTES)
         nc.vector.memset(token_scales[:], 0)
-        first_words = keep.tile([P, PASSES - 1, T], I32, name="first_words", align_bytes=64)
-        last_words = keep.tile([P, T], I32, name="last_words", align_bytes=64)
+        first_words = dma_tile([P, PASSES - 1, T], I32, "first_words", STAGED_BYTES + WORD_BYTES)
+        last_words = dma_tile([P, T], I32, "last_words", STAGED_BYTES)
         token_words = [first_words[:, o, :] for o in range(PASSES - 1)] + [last_words[:]]
-        staged = keep.tile([P, ROW_BLOCKS, RANKS, E * PER_RANK], F32, name="staged")
+        staged = dma_tile([P, ROW_BLOCKS, RANKS, E * PER_RANK], F32, "staged", 0)
         by_rank = out.rearrange("(b p) (m c) -> b p m c", p=P, m=RANKS)
         weights = {}
         slot_words = {}
@@ -69,7 +76,7 @@ def tile_moe_pke_mlp_relu_kernel(tc, x_words, x_scales, w1, w2, offs, out):
         hidden_mx = {}
 
         def ring_tile(step, shape, dtype, name, start=0):
-            return ring.tile(shape, dtype, name=name, offset=(step % RING) * SLOT_BYTES + start, align_bytes=64)
+            return ring.tile(shape, dtype, name=name, offset=(step % RING) * SLOT_BYTES + start, align_bytes=ROW_ALIGN)
 
         def slots_of(first, count):
             return offsets[:, first * C // LIST_GROUP : (first + count) * C // LIST_GROUP]

@@ -34,8 +34,8 @@ LIST_ALIGN = 256
 
 SCALAR_GROUPS = 68
 EARLY = 4
-WHOLE_BLOCKS = [0]
-SPLIT_BLOCKS = [2, 3, 1]
+PAIRED = [0, 1]
+SINGLES = [[2], [3]]
 WHOLE_LOADS = 5
 PROMPT_RELUS = 3
 GATHER_EXPERTS = 3
@@ -52,6 +52,7 @@ def tile_moe_pke_mlp_relu_kernel(tc, x_words, x_scales, w1, w2, offs, out):
         ring = ctx.enter_context(tc.tile_pool(name="ring", bufs=1))
         rounded_pool = ctx.enter_context(tc.tile_pool(name="rounded", bufs=ROUNDED_BUFS))
         code_pool = ctx.enter_context(tc.tile_pool(name="codes", bufs=CODE_BUFS))
+        late = ctx.enter_context(tc.tile_pool(name="late", bufs=1))
         psum = ctx.enter_context(tc.psum_pool(name="psum", bufs=PSUM_BUFS))
 
         def dma_tile(shape, dtype, name, start):
@@ -60,14 +61,11 @@ def tile_moe_pke_mlp_relu_kernel(tc, x_words, x_scales, w1, w2, offs, out):
         offsets = keep.tile([P, E * C // LIST_GROUP], U16, name="offsets", align_bytes=LIST_ALIGN)
         nc.sync.dma_start(offsets[:], offs)
 
-        token_scales = keep.tile([P, T // 4], I32, name="token_scales", align_bytes=64)
         landed_scales = dma_tile([P, T // 4], I32, "landed_scales", STAGED_BYTES + PASSES * WORD_BYTES)
-        nc.vector.memset(token_scales[:], 0)
         first_words = dma_tile([P, PASSES - 1, T], I32, "first_words", STAGED_BYTES + WORD_BYTES)
         last_words = dma_tile([P, T], I32, "last_words", STAGED_BYTES)
         token_words = [first_words[:, o, :] for o in range(PASSES - 1)] + [last_words[:]]
         staged = dma_tile([P, ROW_BLOCKS, RANKS, E * PER_RANK], F32, "staged", 0)
-        by_rank = out.rearrange("(b p) (m c) -> b p m c", p=P, m=RANKS)
         weights = {}
         slot_words = {}
         slot_scales = {}
@@ -84,12 +82,15 @@ def tile_moe_pke_mlp_relu_kernel(tc, x_words, x_scales, w1, w2, offs, out):
         def load_scales():
             for q in range(P // QUADRANT):
                 live = slice(QUADRANT * q, QUADRANT * q + 4 * PASSES)
-                nc.gpsimd.dma_start(out=landed_scales[live, :], in_=x_scales[:, 4 * q : 4 * q + 4, :].bitcast(I32))
+                nc.sync.dma_start(out=landed_scales[live, :], in_=x_scales[:, 4 * q : 4 * q + 4, :].bitcast(I32))
 
         def move_scales():
+            token_scales = dma_tile([P, T // 4], I32, "token_scales", 0)
+            nc.vector.memset(token_scales[:], 0)
             for q in range(P // QUADRANT):
                 live = slice(QUADRANT * q, QUADRANT * q + 4 * PASSES)
                 nc.vector.tensor_copy(out=token_scales[live, :], in_=landed_scales[live, :])
+            return token_scales
 
         def load_expert(step, e):
             raw = ring_tile(step, [P, PASSES, PACK, H], F32, "raw%d" % step)
@@ -102,8 +103,9 @@ def tile_moe_pke_mlp_relu_kernel(tc, x_words, x_scales, w1, w2, offs, out):
             nc.sync.dma_start(out=raw[:], in_=rows.rearrange("(p j) w -> p j w", j=PACK))
             return raw[:]
 
-        def round_columns(raw, first, width, permute, scalar_groups):
-            rounded = rounded_pool.tile([P, width * PACK], BF16, name="rounded", align_bytes=64)
+        def round_columns(raw, first, width, permute, scalar_groups, rounded=None):
+            if rounded is None:
+                rounded = rounded_pool.tile([P, width * PACK], BF16, name="rounded", align_bytes=64)
             src = raw[:, :, first : first + width].rearrange("p j (g i) -> p g j i", i=GROUP)
             order = "p (i g j) -> p g j i" if permute else "p (g i j) -> p g j i"
             dst = rounded[:].rearrange(order, i=GROUP, j=PACK)
@@ -112,14 +114,21 @@ def tile_moe_pke_mlp_relu_kernel(tc, x_words, x_scales, w1, w2, offs, out):
             nc.vector.tensor_copy(out=dst[:, scalar_groups:], in_=src[:, scalar_groups:])
             return rounded
 
+        def round_pairs(raw):
+            rounded = rounded_pool.tile([P, 2 * P * PACK], BF16, name="rounded", align_bytes=64)
+            src = raw[:, :, : 2 * P].rearrange("p j (g u b) -> p g j u b", u=2, b=2)
+            nc.vector.tensor_copy(out=rounded[:].rearrange("p (b g u j) -> p g j u b", b=2, u=2, j=PACK), in_=src)
+            return rounded
+
         def quantise(rounded, width):
             codes = code_pool.tile([P, width], U32, name="w_codes", align_bytes=64)
             scales = code_pool.tile([P, width], U8, name="w_scales", align_bytes=64)
             nc.vector.quantize_mx(out=codes[:].bitcast(FP8X4), scales=scales[:], in_=rounded[:])
             return [(codes[:, c : c + P], scales[:, c : c + P]) for c in range(0, width, P)]
 
-        def gather(window, dtype, first, name):
-            part = keep.tile([P, GATHER_EXPERTS * C], dtype, name="%s_%d" % (name, first), align_bytes=64)
+        def gather(window, dtype, first, name, pool=keep, offset=None):
+            shape = [P, GATHER_EXPERTS * C]
+            part = pool.tile(shape, dtype, name="%s_%d" % (name, first), offset=offset, align_bytes=64)
             nc.vector.tensor_copy(part[:], window.bitcast(dtype).indirect(slots_of(first, GATHER_EXPERTS)))
             return {first + i: part[:, i * C : (i + 1) * C] for i in range(GATHER_EXPERTS)}
 
@@ -177,11 +186,15 @@ def tile_moe_pke_mlp_relu_kernel(tc, x_words, x_scales, w1, w2, offs, out):
 
         def store(blocks, first, last):
             cols = slice(first * PER_RANK, last * PER_RANK)
-            for b in blocks:
-                nc.sync.dma_start(out=by_rank[b][:, :, cols], in_=staged[:, b, :, cols])
+            tiles = slice(blocks[0], blocks[-1] + 1)
+            rows = out[blocks[0] * P : (blocks[-1] + 1) * P, :].rearrange("(p b) (m c) -> p (b m) c", p=P, m=RANKS)
+            nc.sync.dma_start(out=rows[:, :, cols], in_=staged[:, tiles, :, cols].rearrange("p b m c -> p (b m) c"))
 
         def second_layer_parts(e, raw, parts):
-            rounded = [round_columns(raw, blocks[0] * P, len(blocks) * P, False, 0) for blocks in parts]
+            rounded = [
+                round_pairs(raw) if blocks == PAIRED else round_columns(raw, blocks[0] * P, len(blocks) * P, False, 0)
+                for blocks in parts
+            ]
             for blocks, part in zip(parts, rounded):
                 second_layer(e, blocks, quantise(part, len(blocks) * P))
 
@@ -200,10 +213,6 @@ def tile_moe_pke_mlp_relu_kernel(tc, x_words, x_scales, w1, w2, offs, out):
             for first in range(0, E, GATHER_EXPERTS):
                 for e, part in gather(token_words[o], U32, first, "slot_words%d" % o).items():
                     slot_words[e, o] = part
-        move_scales()
-        for first in range(0, E, GATHER_EXPERTS):
-            for e, part in gather(token_scales[:], U8, first, "slot_scales").items():
-                slot_scales[e] = part
 
         for step, (e, o) in enumerate(pieces):
             if e >= WHOLE_LOADS or o == PASSES:
@@ -212,17 +221,22 @@ def tile_moe_pke_mlp_relu_kernel(tc, x_words, x_scales, w1, w2, offs, out):
                 if o == 0:
                     expert_pieces = load_expert(step, e)
                 raw = expert_pieces[o]
-            if o < PASSES:
+            if (e, o) == (0, PASSES - 1):
+                rounded = dma_tile([P, H * PACK], BF16, "rounded_first", 0)
+                weights[e, o] = quantise(round_columns(raw, 0, H, True, SCALAR_GROUPS, rounded), H)
+                token_scales = move_scales()
+                slot_scales.update(gather(token_scales[:], U8, 0, "slot_scales"))
+            elif (e, o) == (1, PASSES - 1):
+                rounded = late.tile([P, H * PACK], BF16, name="rounded_second", offset=0, align_bytes=64)
+                weights[e, o] = quantise(round_columns(raw, 0, H, True, SCALAR_GROUPS, rounded), H)
+                slot_scales.update(gather(token_scales[:], U8, GATHER_EXPERTS, "slot_scales", late, 0))
+            elif o < PASSES:
                 weights[e, o] = quantise(round_columns(raw, 0, H, True, SCALAR_GROUPS), H)
-            elif e == EARLY - 1:
-                second_layer_parts(e, raw, [[2], [3]])
-                second_layer_parts(e, raw, [[0, 1]])
-                store(SPLIT_BLOCKS, 0, EARLY)
-            elif e == E - 1:
-                second_layer_parts(e, raw, [[0], [1]])
-                second_layer_parts(e, raw, [[2, 3]])
+            elif e in (EARLY - 1, E - 1):
+                second_layer_parts(e, raw, SINGLES)
+                second_layer_parts(e, raw, [PAIRED])
             else:
-                second_layer_parts(e, raw, [[0, 1], [2, 3]])
+                second_layer_parts(e, raw, [SINGLES[0] + SINGLES[1], PAIRED])
             if step in relu_step:
                 d = relu_step[step]
                 relu(d, step)
@@ -234,5 +248,6 @@ def tile_moe_pke_mlp_relu_kernel(tc, x_words, x_scales, w1, w2, offs, out):
                 d = late_hidden[step]
                 quantise_hidden(d, ring_tile(step, [P, C], U32, "h_codes%d" % d, SLOT_BYTES // 2))
 
-        store(WHOLE_BLOCKS, 0, E)
-        store(sorted(SPLIT_BLOCKS), EARLY, E)
+        for first, last in ((0, EARLY), (EARLY, E)):
+            for blocks in SINGLES + [PAIRED]:
+                store(blocks, first, last)

from contextlib import ExitStack

import concourse.mybir as mybir

K, T, E, C, H, N = 1536, 1536, 6, 256, 512, 512
RANKS = 4
FLOPS = 2 * E * C * (K * H + H * N)

F32 = mybir.dt.float32
BF16 = mybir.dt.bfloat16
I32 = mybir.dt.int32
U32 = mybir.dt.uint32
U16 = mybir.dt.uint16
U8 = mybir.dt.uint8
FP8X4 = mybir.dt.float8_e4m3fn_x4
RELU = mybir.ActivationFunctionType.Relu

P = 128
PACK = 4
K_PASS = P * PACK
PASSES = K // K_PASS
PER_RANK = C // RANKS
HALF = C // 2
ROW_BLOCKS = N // P
LIST_GROUP = 16
QUADRANT = 32

GROUP = 4
SLOT_BYTES = PACK * H * 4
WORD_BYTES = T * 4
STAGED_BYTES = ROW_BLOCKS * E * C * 4
ROW_ALIGN = 2048
LIST_ALIGN = 256

SCALAR_GROUPS = 68
EARLY = 4
PAIRED = [0, 1]
SINGLES = [[2], [3]]
WHOLE_LOADS = 5
PROMPT_RELUS = 3
GATHER_EXPERTS = 3
RING = 15
ROUNDED_BUFS = 5
CODE_BUFS = 9
PSUM_BUFS = 4


def tile_moe_pke_mlp_relu_kernel(tc, x_words, x_scales, w1, w2, offs, out):
    nc = tc.nc
    with ExitStack() as ctx:
        keep = ctx.enter_context(tc.tile_pool(name="keep", bufs=1))
        ring = ctx.enter_context(tc.tile_pool(name="ring", bufs=1))
        rounded_pool = ctx.enter_context(tc.tile_pool(name="rounded", bufs=ROUNDED_BUFS))
        code_pool = ctx.enter_context(tc.tile_pool(name="codes", bufs=CODE_BUFS))
        late = ctx.enter_context(tc.tile_pool(name="late", bufs=1))
        psum = ctx.enter_context(tc.psum_pool(name="psum", bufs=PSUM_BUFS))

        def dma_tile(shape, dtype, name, start):
            return ring.tile(shape, dtype, name=name, offset=RING * SLOT_BYTES + start, align_bytes=ROW_ALIGN)

        offsets = keep.tile([P, E * C // LIST_GROUP], U16, name="offsets", align_bytes=LIST_ALIGN)
        nc.sync.dma_start(offsets[:], offs)

        landed_scales = dma_tile([P, T // 4], I32, "landed_scales", STAGED_BYTES + PASSES * WORD_BYTES)
        first_words = dma_tile([P, PASSES - 1, T], I32, "first_words", STAGED_BYTES + WORD_BYTES)
        last_words = dma_tile([P, T], I32, "last_words", STAGED_BYTES)
        token_words = [first_words[:, o, :] for o in range(PASSES - 1)] + [last_words[:]]
        staged = dma_tile([P, ROW_BLOCKS, RANKS, E * PER_RANK], F32, "staged", 0)
        weights = {}
        slot_words = {}
        slot_scales = {}
        first_sums = {}
        hidden = {}
        hidden_mx = {}

        def ring_tile(step, shape, dtype, name, start=0):
            return ring.tile(shape, dtype, name=name, offset=(step % RING) * SLOT_BYTES + start, align_bytes=ROW_ALIGN)

        def slots_of(first, count):
            return offsets[:, first * C // LIST_GROUP : (first + count) * C // LIST_GROUP]

        def load_scales():
            for q in range(P // QUADRANT):
                live = slice(QUADRANT * q, QUADRANT * q + 4 * PASSES)
                nc.sync.dma_start(out=landed_scales[live, :], in_=x_scales[:, 4 * q : 4 * q + 4, :].bitcast(I32))

        def move_scales():
            token_scales = dma_tile([P, T // 4], I32, "token_scales", 0)
            nc.vector.memset(token_scales[:], 0)
            for q in range(P // QUADRANT):
                live = slice(QUADRANT * q, QUADRANT * q + 4 * PASSES)
                nc.vector.tensor_copy(out=token_scales[live, :], in_=landed_scales[live, :])
            return token_scales

        def load_expert(step, e):
            raw = ring_tile(step, [P, PASSES, PACK, H], F32, "raw%d" % step)
            nc.sync.dma_start(out=raw[:], in_=w1[e].rearrange("(o p j) w -> p o j w", p=P, j=PACK))
            return [raw[:, o] for o in range(PASSES)]

        def load_piece(step, e, o):
            rows = w1[e, o * K_PASS : (o + 1) * K_PASS, :] if o < PASSES else w2[e]
            raw = ring_tile(step, [P, PACK, H], F32, "raw%d" % step)
            nc.sync.dma_start(out=raw[:], in_=rows.rearrange("(p j) w -> p j w", j=PACK))
            return raw[:]

        def round_columns(raw, first, width, permute, scalar_groups, rounded=None):
            if rounded is None:
                rounded = rounded_pool.tile([P, width * PACK], BF16, name="rounded", align_bytes=64)
            src = raw[:, :, first : first + width].rearrange("p j (g i) -> p g j i", i=GROUP)
            order = "p (i g j) -> p g j i" if permute else "p (g i j) -> p g j i"
            dst = rounded[:].rearrange(order, i=GROUP, j=PACK)
            if scalar_groups > 0:
                nc.scalar.copy(out=dst[:, :scalar_groups], in_=src[:, :scalar_groups])
            nc.vector.tensor_copy(out=dst[:, scalar_groups:], in_=src[:, scalar_groups:])
            return rounded

        def round_pairs(raw):
            rounded = rounded_pool.tile([P, 2 * P * PACK], BF16, name="rounded", align_bytes=64)
            src = raw[:, :, : 2 * P].rearrange("p j (g u b) -> p g j u b", u=2, b=2)
            nc.vector.tensor_copy(out=rounded[:].rearrange("p (b g u j) -> p g j u b", b=2, u=2, j=PACK), in_=src)
            return rounded

        def quantise(rounded, width):
            codes = code_pool.tile([P, width], U32, name="w_codes", align_bytes=64)
            scales = code_pool.tile([P, width], U8, name="w_scales", align_bytes=64)
            nc.vector.quantize_mx(out=codes[:].bitcast(FP8X4), scales=scales[:], in_=rounded[:])
            return [(codes[:, c : c + P], scales[:, c : c + P]) for c in range(0, width, P)]

        def gather(window, dtype, first, name, pool=keep, offset=None):
            shape = [P, GATHER_EXPERTS * C]
            part = pool.tile(shape, dtype, name="%s_%d" % (name, first), offset=offset, align_bytes=64)
            nc.vector.tensor_copy(part[:], window.bitcast(dtype).indirect(slots_of(first, GATHER_EXPERTS)))
            return {first + i: part[:, i * C : (i + 1) * C] for i in range(GATHER_EXPERTS)}

        def first_products(e):
            for half in range(2):
                cols = slice(half * HALF, (half + 1) * HALF)
                acc = psum.tile([P, PACK, HALF], F32, name="acc_a")
                for t in range(PACK):
                    for o in range(PASSES):
                        w_codes, w_scales = weights[e, o][t]
                        nc.tensor.matmul_mx(
                            out=acc[:, t, :],
                            lhsT=w_codes.bitcast(FP8X4),
                            lhsT_scale=w_scales,
                            rhs=slot_words[e, o][:, cols].bitcast(FP8X4),
                            rhs_scale=slot_scales[e][4 * o :, cols],
                            start=(o == 0),
                            stop=(o == PASSES - 1),
                        )
                first_sums[e, half] = acc

        def relu(e, step):
            hidden[e] = ring_tile(step, [P, 2, HALF, PACK], BF16, "hidden%d" % e)
            for half in range(2):
                nc.scalar.activation(
                    out=hidden[e][:, half], in_=first_sums[e, half][:].rearrange("p t s -> p s t"), func=RELU
                )

        def quantise_hidden(e, h_codes):
            h_scales = keep.tile([P, C], U8, name="h_scales%d" % e, align_bytes=64)
            nc.vector.quantize_mx(
                out=h_codes[:].bitcast(FP8X4),
                scales=h_scales[:],
                in_=hidden[e][:].rearrange("p h s t -> p (h s t)"),
            )
            hidden_mx[e] = (h_codes, h_scales)

        def second_layer(e, blocks, w_tiles):
            h_codes, h_scales = hidden_mx[e]
            acc = psum.tile([P, len(blocks), C], F32, name="acc_y")
            for i, (w_codes, w_scales) in enumerate(w_tiles):
                nc.tensor.matmul_mx(
                    out=acc[:, i, :],
                    lhsT=w_codes.bitcast(FP8X4),
                    lhsT_scale=w_scales,
                    rhs=h_codes[:].bitcast(FP8X4),
                    rhs_scale=h_scales[:],
                    start=True,
                    stop=True,
                )
            nc.scalar.copy(
                out=staged[:, blocks[0] : blocks[0] + len(blocks), :, e * PER_RANK : (e + 1) * PER_RANK],
                in_=acc[:].rearrange("p b (m u) -> p b m u", m=RANKS),
            )

        def store(blocks, first, last):
            cols = slice(first * PER_RANK, last * PER_RANK)
            tiles = slice(blocks[0], blocks[-1] + 1)
            rows = out[blocks[0] * P : (blocks[-1] + 1) * P, :].rearrange("(p b) (m c) -> p (b m) c", p=P, m=RANKS)
            nc.sync.dma_start(out=rows[:, :, cols], in_=staged[:, tiles, :, cols].rearrange("p b m c -> p (b m) c"))

        def second_layer_parts(e, raw, parts):
            rounded = [
                round_pairs(raw) if blocks == PAIRED else round_columns(raw, blocks[0] * P, len(blocks) * P, False, 0)
                for blocks in parts
            ]
            for blocks, part in zip(parts, rounded):
                second_layer(e, blocks, quantise(part, len(blocks) * P))

        pieces = [(e, o) for e in range(E) for o in range(PASSES)] + [(e, PASSES) for e in range(E)]
        last_w1 = E * PASSES - 1
        relu_step = {pieces.index((e + 1, PASSES - 1)): e for e in range(PROMPT_RELUS)}
        for e in range(PROMPT_RELUS, E):
            relu_step[last_w1 + e - PROMPT_RELUS] = e
        late_hidden = {step + (1 if e < E - 1 else 2): e for step, e in relu_step.items() if e >= PROMPT_RELUS}

        packed = x_words.rearrange("o p t r -> p o (t r)").bitcast(I32)
        nc.sync.dma_start(out=last_words[:], in_=packed[:, PASSES - 1])
        nc.sync.dma_start(out=first_words[:], in_=packed[:, : PASSES - 1])
        load_scales()
        for o in reversed(range(PASSES)):
            for first in range(0, E, GATHER_EXPERTS):
                for e, part in gather(token_words[o], U32, first, "slot_words%d" % o).items():
                    slot_words[e, o] = part

        for step, (e, o) in enumerate(pieces):
            if e >= WHOLE_LOADS or o == PASSES:
                raw = load_piece(step, e, o)
            else:
                if o == 0:
                    expert_pieces = load_expert(step, e)
                raw = expert_pieces[o]
            if (e, o) == (0, PASSES - 1):
                rounded = dma_tile([P, H * PACK], BF16, "rounded_first", 0)
                weights[e, o] = quantise(round_columns(raw, 0, H, True, SCALAR_GROUPS, rounded), H)
                token_scales = move_scales()
                slot_scales.update(gather(token_scales[:], U8, 0, "slot_scales"))
            elif (e, o) == (1, PASSES - 1):
                rounded = late.tile([P, H * PACK], BF16, name="rounded_second", offset=0, align_bytes=64)
                weights[e, o] = quantise(round_columns(raw, 0, H, True, SCALAR_GROUPS, rounded), H)
                slot_scales.update(gather(token_scales[:], U8, GATHER_EXPERTS, "slot_scales", late, 0))
            elif o < PASSES:
                weights[e, o] = quantise(round_columns(raw, 0, H, True, SCALAR_GROUPS), H)
            elif e in (EARLY - 1, E - 1):
                second_layer_parts(e, raw, SINGLES)
                second_layer_parts(e, raw, [PAIRED])
            else:
                second_layer_parts(e, raw, [SINGLES[0] + SINGLES[1], PAIRED])
            if step in relu_step:
                d = relu_step[step]
                relu(d, step)
                if d < PROMPT_RELUS:
                    quantise_hidden(d, keep.tile([P, C], U32, name="h_codes%d" % d, align_bytes=64))
            if o == PASSES - 1:
                first_products(e)
            if step in late_hidden:
                d = late_hidden[step]
                quantise_hidden(d, ring_tile(step, [P, C], U32, "h_codes%d" % d, SLOT_BYTES // 2))

        for first, last in ((0, EARLY), (EARLY, E)):
            for blocks in SINGLES + [PAIRED]:
                store(blocks, first, last)
